import numpy as np
import ml_dtypes


def mxq(x, axis, fmt="e4m3"):
    dtype, down = {"e4m3": (ml_dtypes.float8_e4m3fn, 7), "e5m2": (ml_dtypes.float8_e5m2, 14)}[fmt]
    v = np.moveaxis(np.asarray(x, np.float32).astype(ml_dtypes.bfloat16).astype(np.float64), axis, -1)
    blocks = v.reshape(v.shape[:-1] + (-1, 32))
    amax = np.abs(blocks).max(-1, keepdims=True)
    byte = np.maximum(np.where(amax > 0, np.frexp(amax)[1] - 1 + 127, 0) - down, 1)
    scale = np.exp2(byte - 127.0)
    codes = (blocks / scale).astype(np.float32).astype(dtype).astype(np.float64)
    return np.moveaxis((codes * scale).reshape(v.shape), -1, axis)


WIDE = False


def mx_kscale(k):
    if not WIDE:
        return np.ones(k)
    levels = np.array([10, -10, 5, -5, 0])
    if k % 512:
        return np.exp2(np.random.permutation(np.resize(levels, k // 32))).repeat(32)
    a = np.empty((k // 512, 16))
    for p in range(k // 512):
        a[p, :8] = np.random.permutation(np.resize(levels, 8))
        for g in range(8):
            far = levels[np.abs(levels - a[p, g]) >= 10]
            a[p, g + 8] = far[np.random.randint(len(far))]
    return np.exp2(a.ravel()).repeat(32)


def f64(x):
    return np.asarray(x).astype(np.float64)


def striped(idx):
    return np.tile(idx.reshape(-1, 16).T, (8, 1)).astype(np.uint16)


def unstriped(offs):
    return offs[:16].T.reshape(-1).astype(np.int64)


def pack_weight(w):
    k, n = w.shape
    w = f64(np.asarray(w, np.float32).astype(ml_dtypes.bfloat16)).reshape(k // 32, 32, n)
    amax = np.abs(w).max(1)
    byte = np.clip(np.where(amax > 0, np.frexp(amax)[1] - 1 + 127 - 7, 1), 1, 254)
    scaled = (w * np.exp2(127.0 - byte)[:, None, :]).reshape(k, n).astype(np.float32)
    words = np.ascontiguousarray(scaled.reshape(k // 512, 128, 4, n).transpose(0, 1, 3, 2)).astype(ml_dtypes.float8_e4m3fn).view(np.uint8)
    return words, np.ascontiguousarray(byte.astype(np.uint8).reshape(k // 512, 16, n))


def unpack_weight(words, scales):
    g, p, n, _ = words.shape
    vals = np.ascontiguousarray(words).view(ml_dtypes.float8_e4m3fn).astype(np.float64) * np.repeat(np.exp2(scales.astype(np.float64) - 127.0), 8, axis=1)[..., None]
    return vals.transpose(0, 1, 3, 2).reshape(g * 512, n)


def relu(v):
    return np.maximum(v, 0.0)


K, T, S, H, N = 512, 4096, 1024, 512, 256


def setup_inputs():
    n = np.random.standard_normal
    s = mx_kscale(K)[:, None]
    u = mx_kscale(H)
    packed_xT = pack_weight(n((K, T)) * s)
    packed_w2 = pack_weight(n((H, N)) / np.sqrt(H) / u[:, None])
    return {
        "x_words": packed_xT[0],
        "x_scales": packed_xT[1],
        "w1": (n((K, H)) / np.sqrt(K) / s).astype(np.float32),
        "w2_words": packed_w2[0],
        "w2_scales": packed_w2[1],
        "gamma": (np.random.uniform(0.5, 1.5, (H, 1)) * u[:, None]).astype(np.float32),
        "offs": striped(np.random.permutation(T)[:S]),
    }


def reference(x_words, x_scales, w1, w2_words, w2_scales, gamma, offs):
    xq = unpack_weight(x_words, x_scales)[:, unstriped(offs)]
    h = mxq(f64(w1), 0, "e4m3").T @ xq
    hn = (h - h.mean(axis=1, keepdims=True)) / np.sqrt(h.var(axis=1, keepdims=True) + 1e-5)
    z = relu(f64(gamma) * hn)
    return unpack_weight(w2_words, w2_scales).T @ mxq(z, 0, "e4m3")

@@ -1,0 +1,244 @@
+from contextlib import ExitStack
+
+import concourse.mybir as mybir
+
+K, T, S, H, N = 512, 4096, 1024, 512, 256
+FLOPS = 2 * K * H * S + 2 * H * N * S
+EPS = 1e-5
+
+F32 = mybir.dt.float32
+BF16 = mybir.dt.bfloat16
+I32 = mybir.dt.int32
+U32 = mybir.dt.uint32
+U16 = mybir.dt.uint16
+U8 = mybir.dt.uint8
+FP8X4 = mybir.dt.float8_e4m3fn_x4
+ACT = mybir.ActivationFunctionType
+ALU = mybir.AluOpType
+
+P = 128
+PACK = 4
+HALF = 512
+QUARTER = 256
+
+
+def tile_picked_inorm_relu_p_kernel(
+    tc, x_words, x_scales, w1, w2_words, w2_scales, gamma, offs, out
+):
+    nc = tc.nc
+    with ExitStack() as ctx:
+        keep = ctx.enter_context(tc.tile_pool(name="keep", bufs=1))
+        psum = ctx.enter_context(tc.psum_pool(name="psum", bufs=1))
+
+        offsets = keep.tile([P, S // 16], U16, name="offsets")
+        xs_table = keep.tile([P, T], U8, name="xs_table", tag="scale_rows", align_bytes=64)
+        xw_table = keep.tile([P, T], I32, name="xw_table", align_bytes=64)
+        w1_raw = keep.tile([P, PACK, H], F32, name="w1_raw", align_bytes=64)
+        w2_codes = keep.tile([P, N], I32, name="w2_codes", align_bytes=64)
+        gain = keep.tile([P, PACK], F32, name="gain")
+
+        xs = keep.tile([P, S], U8, name="xs", align_bytes=64)
+        nc.vector.memset(xs_table[0:112, :].bitcast(I32), 0)
+        nc.vector.memset(xs[:].bitcast(I32), 0)
+
+        warm = keep.tile([P, 2], F32, name="warm")
+        nc.vector.memset(warm[:, 0:1], 1.0)
+        nc.scalar.activation(out=warm[:, 1:2], in_=warm[:, 0:1], func=ACT.Abs_reciprocal_sqrt, bias=EPS)
+
+        nc.sync.dma_start(out=offsets[:], in_=offs)
+        nc.sync.dma_start(out=xs_table[112:128, :].bitcast(I32), in_=x_scales[0].bitcast(I32))
+        nc.sync.dma_start(out=w1_raw[:], in_=w1.rearrange("(p j) c -> p j c", j=PACK))
+        nc.sync.dma_start(out=xw_table[:], in_=x_words[0].rearrange("p n r -> p (n r)").bitcast(I32))
+        nc.sync.dma_start(out=gain[:], in_=gamma.rearrange("(p t) o -> p (t o)", t=PACK))
+        nc.sync.dma_start(out=w2_codes[:], in_=w2_words[0].rearrange("p n r -> p (n r)").bitcast(I32))
+
+        xs_picked = keep.tile([P, S], U8, name="xs_picked", align_bytes=64)
+        nc.vector.tensor_copy(out=xs_picked[:], in_=xs_table[:].indirect(offsets[:]))
+        for q in range(4):
+            nc.scalar.dma_start(
+                out=xs[32 * q : 32 * q + 4, :].bitcast(I32),
+                in_=xs_picked[112 + 4 * q : 116 + 4 * q, :].bitcast(I32),
+            )
+
+        w2_plane = keep.tile([P, N], U8, name="w2_plane", tag="scale_rows", align_bytes=64)
+        nc.vector.memset(w2_plane[:].bitcast(I32), 0)
+        for q in range(4):
+            nc.sync.dma_start(
+                out=w2_plane[32 * q : 32 * q + 4, :].bitcast(I32),
+                in_=w2_scales[0, 4 * q : 4 * q + 4, :].bitcast(I32),
+            )
+
+        w1_grouped = keep.tile([P, PACK, P, PACK], BF16, name="w1_grouped", align_bytes=64)
+        nc.vector.tensor_copy(
+            out=w1_grouped[:].rearrange("p t m j -> p m t j"),
+            in_=w1_raw[:].rearrange("p j (m t) -> p m t j", t=PACK),
+        )
+        w1_codes = keep.tile([P, H], U32, name="w1_codes", align_bytes=64)
+        w1_plane = keep.tile([P, H], U8, name="w1_plane", align_bytes=64)
+        nc.vector.quantize_mx(
+            out=w1_codes[:].bitcast(FP8X4),
+            scales=w1_plane[:],
+            in_=w1_grouped[:].rearrange("p t m j -> p (t m j)"),
+        )
+
+        xw = []
+        for h in range(2):
+            picked = keep.tile([P, HALF], U32, name=f"xw{h}", align_bytes=64)
+            nc.vector.tensor_copy(
+                out=picked[:], in_=xw_table[:].bitcast(U32).indirect(offsets[:, 32 * h : 32 * (h + 1)])
+            )
+            xw.append(picked)
+
+        pairs = keep.tile([P, PACK, 2], F32, name="pairs")
+        minus_gain = keep.tile([P, PACK], F32, name="minus_gain")
+        nc.scalar.activation(out=pairs[:, :, 0], in_=gain[:], func=ACT.Copy)
+        nc.scalar.activation(out=minus_gain[:], in_=gain[:], func=ACT.Copy, scale=-1.0)
+
+        banks = {}
+        for t, h in ((3, 0), (0, 0), (0, 1), (1, 0), (1, 1), (2, 0), (2, 1), (3, 1)):
+            bank = psum.tile([P, HALF], F32, name=f"h{t}{h}", tag=f"bank{2 * t + h}")
+            nc.tensor.matmul_mx(
+                out=bank[:],
+                lhsT=w1_codes[:, P * t : P * (t + 1)].bitcast(FP8X4),
+                lhsT_scale=w1_plane[:, P * t : P * (t + 1)],
+                rhs=xw[h][:].bitcast(FP8X4),
+                rhs_scale=xs[:, HALF * h : HALF * (h + 1)],
+                start=True,
+                stop=True,
+            )
+            banks[t, h] = bank
+
+        planes = [keep.tile([P, PACK, HALF], BF16, name=f"planes{h}", align_bytes=64) for h in range(2)]
+        stats = [keep.tile([P, 12], F32, name=f"stats{t}") for t in range(PACK)]
+        scratch = keep.tile([P, 2, QUARTER], BF16, name="scratch")
+
+        def measure_on_scalar(t):
+            nc.vector.memset(stats[t][:, 0:6], float(QUARTER))
+            for g in range(2):
+                nc.scalar.activation(
+                    out=scratch[:, g, :], in_=banks[t, 0][:, QUARTER * g : QUARTER * (g + 1)], func=ACT.Identity,
+                    scale=1.0 / QUARTER, accum_out=stats[t][:, 3 * g + 1 : 3 * g + 2],
+                )
+            for g in range(2):
+                nc.scalar.activation(
+                    out=scratch[:, g, :], in_=banks[t, 0][:, QUARTER * g : QUARTER * (g + 1)], func=ACT.Square,
+                    scale=-1.0, bias=stats[t][:, 3 * g + 1 : 3 * g + 2], accum_out=stats[t][:, 3 * g + 2 : 3 * g + 3],
+                )
+
+        moments = [keep.tile([P, 2], F32, name=f"moments{t}") for t in range(PACK)]
+        rstd = [keep.tile([P, 1], F32, name=f"rstd{t}") for t in range(PACK)]
+        affine = [keep.tile([P, 2], F32, name=f"affine{t}") for t in range(PACK)]
+
+        def measure(t, h):
+            nc.vector.bn_stats(out=stats[t][:, 6 * h : 6 * (h + 1)], in_=banks[t, h][:])
+
+        def aggregate(t):
+            nc.vector.bn_aggr(out=moments[t][:], in_=stats[t][:])
+
+        def factors(t):
+            nc.scalar.activation(out=rstd[t][:], in_=moments[t][:, 1:2], func=ACT.Abs_reciprocal_sqrt, bias=EPS)
+            nc.scalar.activation(
+                out=pairs[:, t, 1:2], in_=moments[t][:, 0:1], func=ACT.Copy, scale=minus_gain[:, t : t + 1]
+            )
+
+        def combine(t):
+            nc.scalar.activation(out=affine[t][:], in_=pairs[:, t, :], func=ACT.Copy, scale=rstd[t][:])
+
+        def normalise(engine, t, n0, width):
+            h, c0 = divmod(n0, HALF)
+            if engine == "vector":
+                nc.vector.tensor_scalar(
+                    out=planes[h][:, t, c0 : c0 + width], in0=banks[t, h][:, c0 : c0 + width],
+                    scalar1=affine[t][:, 0:1], scalar2=affine[t][:, 1:2], op0=ALU.mult, op1=ALU.add,
+                )
+            else:
+                nc.scalar.activation(
+                    out=planes[h][:, t, c0 : c0 + width], in_=banks[t, h][:, c0 : c0 + width], func=ACT.Relu,
+                    scale=affine[t][:, 0:1], bias=affine[t][:, 1:2],
+                )
+
+        measure_on_scalar(3)
+        measure(0, 0)
+        measure(0, 1)
+        measure(1, 0)
+        aggregate(0)
+        factors(0)
+        combine(0)
+        measure(1, 1)
+        normalise("scalar", 0, 0, HALF)
+        measure(2, 0)
+        aggregate(1)
+        factors(1)
+        normalise("scalar", 0, HALF, HALF)
+        combine(1)
+        measure(2, 1)
+        measure(3, 1)
+        normalise("scalar", 1, 0, HALF)
+        aggregate(2)
+        aggregate(3)
+        factors(2)
+        factors(3)
+        combine(2)
+        combine(3)
+        normalise("vector", 1, HALF, HALF)
+        normalise("vector", 2, 0, HALF)
+        normalise("scalar", 3, 0, QUARTER)
+        normalise("scalar", 3, QUARTER, QUARTER)
+        normalise("scalar", 2, HALF, HALF)
+        normalise("scalar", 3, HALF, QUARTER)
+        normalise("scalar", 3, HALF + QUARTER, QUARTER)
+
+        out_view = out.rearrange("(a p) n -> p a n", p=P)
+        pieces = ((0, 256), (256, 256), (512, 256), (768, 128), (896, 128))
+        grouped = {}
+
+        def weave(engine, q):
+            n0, width = pieces[q]
+            h, c0 = divmod(n0, HALF)
+            grouped[q] = keep.tile([P, width, PACK], BF16, name=f"z_grouped{q}", align_bytes=64)
+            dst = grouped[q][:].rearrange("p (c i) t -> p c t i", i=4)
+            src = planes[h][:, :, c0 : c0 + width].rearrange("p t (c i) -> p c t i", i=4)
+            if engine == "scalar":
+                nc.scalar.activation(out=dst, in_=src, func=ACT.Relu)
+            else:
+                nc.vector.tensor_scalar(out=dst, in0=src, scalar1=0.0, scalar2=None, op0=ALU.max)
+
+        def finish(q):
+            n0, width = pieces[q]
+            last = q == len(pieces) - 1
+            z_codes = keep.tile([P, width], U32, name=f"z_codes{q}", align_bytes=64)
+            z_plane = keep.tile([P, width], U8, name=f"z_plane{q}", align_bytes=64)
+            nc.vector.quantize_mx(
+                out=z_codes[:].bitcast(FP8X4), scales=z_plane[:], in_=grouped[q][:].rearrange("p n t -> p (n t)")
+            )
+            result = keep.tile([P, 2, width], F32, name=f"result{q}")
+            acc = psum.tile([P, 2, width], F32, name=f"acc{q}", tag=f"bank{(0, 1, 2, 3, 4, 6)[q]}")
+            spare = psum.tile([P, width], F32, name="spare", tag="bank7") if last else None
+            for a in range(2):
+                target = spare[:] if last and a == 1 else acc[:, a, :]
+                nc.tensor.matmul_mx(
+                    out=target,
+                    lhsT=w2_codes[:, P * a : P * (a + 1)].bitcast(FP8X4),
+                    lhsT_scale=w2_plane[:, P * a : P * (a + 1)],
+                    rhs=z_codes[:].bitcast(FP8X4),
+                    rhs_scale=z_plane[:],
+                    start=True,
+                    stop=True,
+                )
+            if last:
+                nc.scalar.copy(out=result[:, 0, :], in_=acc[:, 0, :])
+                nc.vector.tensor_copy(out=result[:, 1, :], in_=spare[:])
+            else:
+                nc.scalar.copy(out=result[:], in_=acc[:])
+            nc.sync.dma_start(out=out_view[:, :, n0 : n0 + width], in_=result[:])
+
+        weave("vector", 0)
+        weave("vector", 1)
+        finish(0)
+        weave("scalar", 4)
+        weave("vector", 2)
+        finish(1)
+        weave("vector", 3)
+        finish(2)
+        finish(3)
+        finish(4)

@@ -48,9 +48,11 @@ def tile_picked_inorm_relu_p_kernel(
         nc.sync.dma_start(out=offsets[:], in_=offs)
         nc.sync.dma_start(out=xs_table[112:128, :].bitcast(I32), in_=x_scales[0].bitcast(I32))
         nc.sync.dma_start(out=w1_raw[:], in_=w1.rearrange("(p j) c -> p j c", j=PACK))
-        nc.sync.dma_start(out=xw_table[:], in_=x_words[0].rearrange("p n r -> p (n r)").bitcast(I32))
-        nc.sync.dma_start(out=gain[:], in_=gamma.rearrange("(p t) o -> p (t o)", t=PACK))
+        x_rows = x_words[0].rearrange("p n r -> p (n r)").bitcast(I32)
+        nc.sync.dma_start(out=xw_table[:, :3072], in_=x_rows[:, :3072], max_dma_last_dim=4096)
         nc.sync.dma_start(out=w2_codes[:], in_=w2_words[0].rearrange("p n r -> p (n r)").bitcast(I32))
+        nc.sync.dma_start(out=xw_table[:, 3072:], in_=x_rows[:, 3072:])
+        nc.sync.dma_start(out=gain[:], in_=gamma.rearrange("(p t) o -> p (t o)", t=PACK))
 
         xs_picked = keep.tile([P, S], U8, name="xs_picked", align_bytes=64)
         nc.vector.tensor_copy(out=xs_picked[:], in_=xs_table[:].indirect(offsets[:]))
@@ -69,10 +71,10 @@ def tile_picked_inorm_relu_p_kernel(
             )
 
         w1_grouped = keep.tile([P, PACK, P, PACK], BF16, name="w1_grouped", align_bytes=64)
-        nc.vector.tensor_copy(
-            out=w1_grouped[:].rearrange("p t m j -> p m t j"),
-            in_=w1_raw[:].rearrange("p j (m t) -> p m t j", t=PACK),
-        )
+        w1_dst = w1_grouped[:].rearrange("p t m j -> p m t j")
+        w1_src = w1_raw[:].rearrange("p j (m t) -> p m t j", t=PACK)
+        nc.scalar.copy(out=w1_dst[:, 0:64], in_=w1_src[:, 0:64])
+        nc.vector.tensor_copy(out=w1_dst[:, 64:128], in_=w1_src[:, 64:128])
         w1_codes = keep.tile([P, H], U32, name="w1_codes", align_bytes=64)
         w1_plane = keep.tile([P, H], U8, name="w1_plane", align_bytes=64)
         nc.vector.quantize_mx(
@@ -94,8 +96,20 @@ def tile_picked_inorm_relu_p_kernel(
         nc.scalar.activation(out=pairs[:, :, 0], in_=gain[:], func=ACT.Copy)
         nc.scalar.activation(out=minus_gain[:], in_=gain[:], func=ACT.Copy, scale=-1.0)
 
+        idle = psum.tile([P, HALF], F32, name="idle", tag="bank7")
+        for turn in range(3):
+            nc.tensor.matmul_mx(
+                out=idle[:],
+                lhsT=w2_codes[:, 0:P].bitcast(FP8X4),
+                lhsT_scale=w1_plane[:, 0:P],
+                rhs=w1_codes[:].bitcast(FP8X4),
+                rhs_scale=w1_plane[:],
+                start=True,
+                stop=True,
+            )
+
         banks = {}
-        for t, h in ((3, 0), (0, 0), (0, 1), (1, 0), (1, 1), (2, 0), (2, 1), (3, 1)):
+        for t, h in ((0, 0), (2, 0), (1, 0), (0, 1), (1, 1), (3, 0), (2, 1), (3, 1)):
             bank = psum.tile([P, HALF], F32, name=f"h{t}{h}", tag=f"bank{2 * t + h}")
             nc.tensor.matmul_mx(
                 out=bank[:],
@@ -112,18 +126,19 @@ def tile_picked_inorm_relu_p_kernel(
         stats = [keep.tile([P, 12], F32, name=f"stats{t}") for t in range(PACK)]
         scratch = keep.tile([P, 2, QUARTER], BF16, name="scratch")
 
-        def measure_on_scalar(t):
+        def mean_on_scalar(t):
             nc.vector.memset(stats[t][:, 0:6], float(QUARTER))
             for g in range(2):
                 nc.scalar.activation(
                     out=scratch[:, g, :], in_=banks[t, 0][:, QUARTER * g : QUARTER * (g + 1)], func=ACT.Identity,
                     scale=1.0 / QUARTER, accum_out=stats[t][:, 3 * g + 1 : 3 * g + 2],
                 )
-            for g in range(2):
-                nc.scalar.activation(
-                    out=scratch[:, g, :], in_=banks[t, 0][:, QUARTER * g : QUARTER * (g + 1)], func=ACT.Square,
-                    scale=-1.0, bias=stats[t][:, 3 * g + 1 : 3 * g + 2], accum_out=stats[t][:, 3 * g + 2 : 3 * g + 3],
-                )
+
+        def spread_on_scalar(t, g):
+            nc.scalar.activation(
+                out=scratch[:, g, :], in_=banks[t, 0][:, QUARTER * g : QUARTER * (g + 1)], func=ACT.Square,
+                scale=-1.0, bias=stats[t][:, 3 * g + 1 : 3 * g + 2], accum_out=stats[t][:, 3 * g + 2 : 3 * g + 3],
+            )
 
         moments = [keep.tile([P, 2], F32, name=f"moments{t}") for t in range(PACK)]
         rstd = [keep.tile([P, 1], F32, name=f"rstd{t}") for t in range(PACK)]
@@ -157,39 +172,43 @@ def tile_picked_inorm_relu_p_kernel(
                     scale=affine[t][:, 0:1], bias=affine[t][:, 1:2],
                 )
 
-        measure_on_scalar(3)
-        measure(0, 0)
+        mean_on_scalar(0)
+        measure(2, 0)
+        spread_on_scalar(0, 0)
+        spread_on_scalar(0, 1)
+        mean_on_scalar(1)
         measure(0, 1)
-        measure(1, 0)
         aggregate(0)
+        spread_on_scalar(1, 0)
         factors(0)
+        spread_on_scalar(1, 1)
         combine(0)
         measure(1, 1)
-        normalise("scalar", 0, 0, HALF)
-        measure(2, 0)
+        measure(3, 0)
+        normalise("scalar", 0, 0, 512)
         aggregate(1)
         factors(1)
-        normalise("scalar", 0, HALF, HALF)
+        normalise("scalar", 0, 512, 256)
         combine(1)
+        normalise("scalar", 0, 768, 256)
         measure(2, 1)
         measure(3, 1)
-        normalise("scalar", 1, 0, HALF)
+        normalise("scalar", 1, 0, 512)
         aggregate(2)
         aggregate(3)
         factors(2)
         factors(3)
         combine(2)
         combine(3)
-        normalise("vector", 1, HALF, HALF)
-        normalise("vector", 2, 0, HALF)
-        normalise("scalar", 3, 0, QUARTER)
-        normalise("scalar", 3, QUARTER, QUARTER)
-        normalise("scalar", 2, HALF, HALF)
-        normalise("scalar", 3, HALF, QUARTER)
-        normalise("scalar", 3, HALF + QUARTER, QUARTER)
+        normalise("vector", 1, 512, 512)
+        normalise("vector", 2, 0, 512)
+        normalise("scalar", 3, 0, 256)
+        normalise("scalar", 3, 256, 256)
+        normalise("scalar", 3, 512, 512)
+        normalise("scalar", 2, 512, 512)
 
         out_view = out.rearrange("(a p) n -> p a n", p=P)
-        pieces = ((0, 256), (256, 256), (512, 256), (768, 128), (896, 128))
+        pieces = ((0, 128), (128, 128), (256, 256), (512, 256), (768, 128), (896, 128))
         grouped = {}
 
         def weave(engine, q):
@@ -203,9 +222,8 @@ def tile_picked_inorm_relu_p_kernel(
             else:
                 nc.vector.tensor_scalar(out=dst, in0=src, scalar1=0.0, scalar2=None, op0=ALU.max)
 
-        def finish(q):
+        def finish(q, engine):
             n0, width = pieces[q]
-            last = q == len(pieces) - 1
             z_codes = keep.tile([P, width], U32, name=f"z_codes{q}", align_bytes=64)
             z_plane = keep.tile([P, width], U8, name=f"z_plane{q}", align_bytes=64)
             nc.vector.quantize_mx(
@@ -213,11 +231,9 @@ def tile_picked_inorm_relu_p_kernel(
             )
             result = keep.tile([P, 2, width], F32, name=f"result{q}")
             acc = psum.tile([P, 2, width], F32, name=f"acc{q}", tag=f"bank{(0, 1, 2, 3, 4, 6)[q]}")
-            spare = psum.tile([P, width], F32, name="spare", tag="bank7") if last else None
             for a in range(2):
-                target = spare[:] if last and a == 1 else acc[:, a, :]
                 nc.tensor.matmul_mx(
-                    out=target,
+                    out=acc[:, a, :],
                     lhsT=w2_codes[:, P * a : P * (a + 1)].bitcast(FP8X4),
                     lhsT_scale=w2_plane[:, P * a : P * (a + 1)],
                     rhs=z_codes[:].bitcast(FP8X4),
@@ -225,20 +241,21 @@ def tile_picked_inorm_relu_p_kernel(
                     start=True,
                     stop=True,
                 )
-            if last:
-                nc.scalar.copy(out=result[:, 0, :], in_=acc[:, 0, :])
-                nc.vector.tensor_copy(out=result[:, 1, :], in_=spare[:])
+            if engine == "vector":
+                nc.vector.tensor_copy(out=result[:], in_=acc[:])
             else:
                 nc.scalar.copy(out=result[:], in_=acc[:])
             nc.sync.dma_start(out=out_view[:, :, n0 : n0 + width], in_=result[:])
 
         weave("vector", 0)
         weave("vector", 1)
-        finish(0)
-        weave("scalar", 4)
+        finish(0, "scalar")
+        finish(1, "scalar")
         weave("vector", 2)
-        finish(1)
+        weave("scalar", 5)
         weave("vector", 3)
-        finish(2)
-        finish(3)
-        finish(4)
+        finish(2, "scalar")
+        weave("vector", 4)
+        finish(3, "scalar")
+        finish(5, "scalar")
+        finish(4, "vector")

@@ -48,11 +48,9 @@ def tile_picked_inorm_relu_p_kernel(
         nc.sync.dma_start(out=offsets[:], in_=offs)
         nc.sync.dma_start(out=xs_table[112:128, :].bitcast(I32), in_=x_scales[0].bitcast(I32))
         nc.sync.dma_start(out=w1_raw[:], in_=w1.rearrange("(p j) c -> p j c", j=PACK))
-        x_rows = x_words[0].rearrange("p n r -> p (n r)").bitcast(I32)
-        nc.sync.dma_start(out=xw_table[:, :3072], in_=x_rows[:, :3072], max_dma_last_dim=4096)
-        nc.sync.dma_start(out=w2_codes[:], in_=w2_words[0].rearrange("p n r -> p (n r)").bitcast(I32))
-        nc.sync.dma_start(out=xw_table[:, 3072:], in_=x_rows[:, 3072:])
+        nc.sync.dma_start(out=xw_table[:], in_=x_words[0].rearrange("p n r -> p (n r)").bitcast(I32))
         nc.sync.dma_start(out=gain[:], in_=gamma.rearrange("(p t) o -> p (t o)", t=PACK))
+        nc.sync.dma_start(out=w2_codes[:], in_=w2_words[0].rearrange("p n r -> p (n r)").bitcast(I32))
 
         xs_picked = keep.tile([P, S], U8, name="xs_picked", align_bytes=64)
         nc.vector.tensor_copy(out=xs_picked[:], in_=xs_table[:].indirect(offsets[:]))
@@ -91,25 +89,14 @@ def tile_picked_inorm_relu_p_kernel(
             )
             xw.append(picked)
 
-        pairs = keep.tile([P, PACK, 2], F32, name="pairs")
+        pairs = keep.tile([P, PACK, 3], F32, name="pairs")
         minus_gain = keep.tile([P, PACK], F32, name="minus_gain")
         nc.scalar.activation(out=pairs[:, :, 0], in_=gain[:], func=ACT.Copy)
+        nc.scalar.activation(out=pairs[:, :, 2], in_=gain[:], func=ACT.Copy, scale=float(QUARTER))
         nc.scalar.activation(out=minus_gain[:], in_=gain[:], func=ACT.Copy, scale=-1.0)
 
-        idle = psum.tile([P, HALF], F32, name="idle", tag="bank7")
-        for turn in range(3):
-            nc.tensor.matmul_mx(
-                out=idle[:],
-                lhsT=w2_codes[:, 0:P].bitcast(FP8X4),
-                lhsT_scale=w1_plane[:, 0:P],
-                rhs=w1_codes[:].bitcast(FP8X4),
-                rhs_scale=w1_plane[:],
-                start=True,
-                stop=True,
-            )
-
         banks = {}
-        for t, h in ((0, 0), (2, 0), (1, 0), (0, 1), (1, 1), (3, 0), (2, 1), (3, 1)):
+        for t, h in ((0, 0), (2, 0), (3, 0), (0, 1), (1, 0), (1, 1), (2, 1), (3, 1)):
             bank = psum.tile([P, HALF], F32, name=f"h{t}{h}", tag=f"bank{2 * t + h}")
             nc.tensor.matmul_mx(
                 out=bank[:],
@@ -125,12 +112,13 @@ def tile_picked_inorm_relu_p_kernel(
         planes = [keep.tile([P, PACK, HALF], BF16, name=f"planes{h}", align_bytes=64) for h in range(2)]
         stats = [keep.tile([P, 12], F32, name=f"stats{t}") for t in range(PACK)]
         scratch = keep.tile([P, 2, QUARTER], BF16, name="scratch")
+        shrunk = {t: keep.tile([P, HALF], F32, name=f"shrunk{t}") for t in (0, 1)}
 
         def mean_on_scalar(t):
             nc.vector.memset(stats[t][:, 0:6], float(QUARTER))
             for g in range(2):
                 nc.scalar.activation(
-                    out=scratch[:, g, :], in_=banks[t, 0][:, QUARTER * g : QUARTER * (g + 1)], func=ACT.Identity,
+                    out=shrunk[t][:, QUARTER * g : QUARTER * (g + 1)], in_=banks[t, 0][:, QUARTER * g : QUARTER * (g + 1)], func=ACT.Identity,
                     scale=1.0 / QUARTER, accum_out=stats[t][:, 3 * g + 1 : 3 * g + 2],
                 )
 
@@ -142,7 +130,7 @@ def tile_picked_inorm_relu_p_kernel(
 
         moments = [keep.tile([P, 2], F32, name=f"moments{t}") for t in range(PACK)]
         rstd = [keep.tile([P, 1], F32, name=f"rstd{t}") for t in range(PACK)]
-        affine = [keep.tile([P, 2], F32, name=f"affine{t}") for t in range(PACK)]
+        affine = [keep.tile([P, 3], F32, name=f"affine{t}") for t in range(PACK)]
 
         def measure(t, h):
             nc.vector.bn_stats(out=stats[t][:, 6 * h : 6 * (h + 1)], in_=banks[t, h][:])
@@ -161,7 +149,12 @@ def tile_picked_inorm_relu_p_kernel(
 
         def normalise(engine, t, n0, width):
             h, c0 = divmod(n0, HALF)
-            if engine == "vector":
+            if engine == "copy":
+                nc.vector.tensor_scalar(
+                    out=planes[h][:, t, c0 : c0 + width], in0=shrunk[t][:, c0 : c0 + width],
+                    scalar1=affine[t][:, 2:3], scalar2=affine[t][:, 1:2], op0=ALU.mult, op1=ALU.add,
+                )
+            elif engine == "vector":
                 nc.vector.tensor_scalar(
                     out=planes[h][:, t, c0 : c0 + width], in0=banks[t, h][:, c0 : c0 + width],
                     scalar1=affine[t][:, 0:1], scalar2=affine[t][:, 1:2], op0=ALU.mult, op1=ALU.add,
@@ -176,47 +169,54 @@ def tile_picked_inorm_relu_p_kernel(
         measure(2, 0)
         spread_on_scalar(0, 0)
         spread_on_scalar(0, 1)
-        mean_on_scalar(1)
+        measure(3, 0)
         measure(0, 1)
         aggregate(0)
-        spread_on_scalar(1, 0)
         factors(0)
-        spread_on_scalar(1, 1)
         combine(0)
+        mean_on_scalar(1)
+        spread_on_scalar(1, 0)
+        spread_on_scalar(1, 1)
         measure(1, 1)
-        measure(3, 0)
-        normalise("scalar", 0, 0, 512)
+        measure(2, 1)
         aggregate(1)
         factors(1)
-        normalise("scalar", 0, 512, 256)
         combine(1)
+        normalise("scalar", 0, 512, 256)
         normalise("scalar", 0, 768, 256)
-        measure(2, 1)
         measure(3, 1)
-        normalise("scalar", 1, 0, 512)
         aggregate(2)
         aggregate(3)
         factors(2)
         factors(3)
         combine(2)
         combine(3)
+        normalise("copy", 0, 0, 512)
+        normalise("copy", 1, 0, 512)
         normalise("vector", 1, 512, 512)
-        normalise("vector", 2, 0, 512)
-        normalise("scalar", 3, 0, 256)
+        normalise("scalar", 2, 0, 128)
+        normalise("scalar", 3, 0, 128)
+        normalise("scalar", 2, 128, 128)
+        normalise("scalar", 3, 128, 128)
+        normalise("scalar", 2, 256, 256)
         normalise("scalar", 3, 256, 256)
-        normalise("scalar", 3, 512, 512)
-        normalise("scalar", 2, 512, 512)
+        normalise("scalar", 2, 512, 256)
+        normalise("scalar", 3, 512, 256)
+        normalise("scalar", 2, 768, 256)
+        normalise("scalar", 3, 768, 256)
 
         out_view = out.rearrange("(a p) n -> p a n", p=P)
-        pieces = ((0, 128), (128, 128), (256, 256), (512, 256), (768, 128), (896, 128))
+        pieces = tuple((128 * q, 128) for q in range(8))
         grouped = {}
 
-        def weave(engine, q):
+        def weave(engine, q, lo=0, hi=None):
             n0, width = pieces[q]
+            hi = width if hi is None else hi
             h, c0 = divmod(n0, HALF)
-            grouped[q] = keep.tile([P, width, PACK], BF16, name=f"z_grouped{q}", align_bytes=64)
-            dst = grouped[q][:].rearrange("p (c i) t -> p c t i", i=4)
-            src = planes[h][:, :, c0 : c0 + width].rearrange("p t (c i) -> p c t i", i=4)
+            if q not in grouped:
+                grouped[q] = keep.tile([P, width, PACK], BF16, name=f"z_grouped{q}", align_bytes=64)
+            dst = grouped[q][:, lo:hi, :].rearrange("p (c i) t -> p c t i", i=4)
+            src = planes[h][:, :, c0 + lo : c0 + hi].rearrange("p t (c i) -> p c t i", i=4)
             if engine == "scalar":
                 nc.scalar.activation(out=dst, in_=src, func=ACT.Relu)
             else:
@@ -230,7 +230,7 @@ def tile_picked_inorm_relu_p_kernel(
                 out=z_codes[:].bitcast(FP8X4), scales=z_plane[:], in_=grouped[q][:].rearrange("p n t -> p (n t)")
             )
             result = keep.tile([P, 2, width], F32, name=f"result{q}")
-            acc = psum.tile([P, 2, width], F32, name=f"acc{q}", tag=f"bank{(0, 1, 2, 3, 4, 6)[q]}")
+            acc = psum.tile([P, 2, width], F32, name=f"acc{q}", tag=f"bank{(0, 2, 1, 3, 4, 6, 7, 5)[q]}")
             for a in range(2):
                 nc.tensor.matmul_mx(
                     out=acc[:, a, :],
@@ -250,12 +250,16 @@ def tile_picked_inorm_relu_p_kernel(
         weave("vector", 0)
         weave("vector", 1)
         finish(0, "scalar")
-        finish(1, "scalar")
         weave("vector", 2)
-        weave("scalar", 5)
+        finish(1, "scalar")
+        weave("scalar", 7)
         weave("vector", 3)
         finish(2, "scalar")
         weave("vector", 4)
         finish(3, "scalar")
-        finish(5, "scalar")
-        finish(4, "vector")
+        weave("vector", 5)
+        finish(4, "scalar")
+        weave("vector", 6)
+        finish(5, "vector")
+        finish(7, "scalar")
+        finish(6, "vector")

@@ -95,6 +95,18 @@ def tile_picked_inorm_relu_p_kernel(
         nc.scalar.activation(out=pairs[:, :, 2], in_=gain[:], func=ACT.Copy, scale=float(QUARTER))
         nc.scalar.activation(out=minus_gain[:], in_=gain[:], func=ACT.Copy, scale=-1.0)
 
+        idle = psum.tile([P, HALF], F32, name="idle", tag="bank7")
+        for turn in range(3):
+            nc.tensor.matmul_mx(
+                out=idle[:],
+                lhsT=w1_codes[:, 0:P].bitcast(FP8X4),
+                lhsT_scale=w1_plane[:, 0:P],
+                rhs=w1_codes[:].bitcast(FP8X4),
+                rhs_scale=w1_plane[:],
+                start=True,
+                stop=True,
+            )
+
         banks = {}
         for t, h in ((0, 0), (2, 0), (3, 0), (0, 1), (1, 0), (1, 1), (2, 1), (3, 1)):
             bank = psum.tile([P, HALF], F32, name=f"h{t}{h}", tag=f"bank{2 * t + h}")

@@ -38,29 +38,33 @@ def tile_picked_inorm_relu_p_kernel(
         gain = keep.tile([P, PACK], F32, name="gain")
 
         xs = keep.tile([P, S], U8, name="xs", align_bytes=64)
-        nc.vector.memset(xs_table[0:112, :].bitcast(I32), 0)
+        nc.vector.memset(xs_table[:].bitcast(I32), 0)
         nc.vector.memset(xs[:].bitcast(I32), 0)
 
         warm = keep.tile([P, 2], F32, name="warm")
         nc.vector.memset(warm[:, 0:1], 1.0)
         nc.scalar.activation(out=warm[:, 1:2], in_=warm[:, 0:1], func=ACT.Abs_reciprocal_sqrt, bias=EPS)
 
-        nc.sync.dma_start(out=offsets[:], in_=offs)
-        nc.sync.dma_start(out=xs_table[112:128, :].bitcast(I32), in_=x_scales[0].bitcast(I32))
         nc.sync.dma_start(out=w1_raw[:], in_=w1.rearrange("(p j) c -> p j c", j=PACK))
+        nc.sync.dma_start(out=offsets[:], in_=offs)
+        for u in range(2):
+            nc.sync.dma_start(
+                out=xs_table[64 * u : 64 * u + 32 : 4, :].bitcast(I32),
+                in_=x_scales[0, 8 * u : 8 * u + 8, :].bitcast(I32),
+            )
         nc.sync.dma_start(out=xw_table[:], in_=x_words[0].rearrange("p n r -> p (n r)").bitcast(I32))
         nc.sync.dma_start(out=gain[:], in_=gamma.rearrange("(p t) o -> p (t o)", t=PACK))
         nc.sync.dma_start(out=w2_codes[:], in_=w2_words[0].rearrange("p n r -> p (n r)").bitcast(I32))
 
-        xs_picked = keep.tile([P, S], U8, name="xs_picked", align_bytes=64)
+        xs_picked = keep.tile([P, S], U8, name="xs_picked", tag="picked_rows", align_bytes=64)
         nc.vector.tensor_copy(out=xs_picked[:], in_=xs_table[:].indirect(offsets[:]))
         for q in range(4):
             nc.scalar.dma_start(
                 out=xs[32 * q : 32 * q + 4, :].bitcast(I32),
-                in_=xs_picked[112 + 4 * q : 116 + 4 * q, :].bitcast(I32),
+                in_=xs_picked[64 * (q // 2) + 16 * (q % 2) : 64 * (q // 2) + 16 * (q % 2) + 16 : 4, :].bitcast(I32),
             )
 
-        w2_plane = keep.tile([P, N], U8, name="w2_plane", tag="scale_rows", align_bytes=64)
+        w2_plane = keep.tile([P, N], U8, name="w2_plane", tag="picked_rows", align_bytes=64)
         nc.vector.memset(w2_plane[:].bitcast(I32), 0)
         for q in range(4):
             nc.sync.dma_start(
@@ -71,9 +75,8 @@ def tile_picked_inorm_relu_p_kernel(
         w1_grouped = keep.tile([P, PACK, P, PACK], BF16, name="w1_grouped", align_bytes=64)
         w1_dst = w1_grouped[:].rearrange("p t m j -> p m t j")
         w1_src = w1_raw[:].rearrange("p j (m t) -> p m t j", t=PACK)
-        nc.scalar.copy(out=w1_dst[:, 0:64], in_=w1_src[:, 0:64])
-        nc.vector.tensor_copy(out=w1_dst[:, 64:128], in_=w1_src[:, 64:128])
-        w1_codes = keep.tile([P, H], U32, name="w1_codes", align_bytes=64)
+        nc.scalar.copy(out=w1_dst, in_=w1_src)
+        w1_codes = keep.tile([P, H], U32, name="w1_codes", tag="scale_rows", align_bytes=64)
         w1_plane = keep.tile([P, H], U8, name="w1_plane", align_bytes=64)
         nc.vector.quantize_mx(
             out=w1_codes[:].bitcast(FP8X4),
@@ -96,7 +99,7 @@ def tile_picked_inorm_relu_p_kernel(
         nc.scalar.activation(out=minus_gain[:], in_=gain[:], func=ACT.Copy, scale=-1.0)
 
         idle = psum.tile([P, HALF], F32, name="idle", tag="bank7")
-        for turn in range(3):
+        for turn in range(2):
             nc.tensor.matmul_mx(
                 out=idle[:],
                 lhsT=w1_codes[:, 0:P].bitcast(FP8X4),

@@ -20,6 +20,7 @@ P = 128
 PACK = 4
 HALF = 512
 QUARTER = 256
+SCALAR_TILES = (0, 1)
 
 
 def tile_picked_inorm_relu_p_kernel(
@@ -47,11 +48,7 @@ def tile_picked_inorm_relu_p_kernel(
 
         nc.sync.dma_start(out=w1_raw[:], in_=w1.rearrange("(p j) c -> p j c", j=PACK))
         nc.sync.dma_start(out=offsets[:], in_=offs)
-        for u in range(2):
-            nc.sync.dma_start(
-                out=xs_table[64 * u : 64 * u + 32 : 4, :].bitcast(I32),
-                in_=x_scales[0, 8 * u : 8 * u + 8, :].bitcast(I32),
-            )
+        nc.sync.dma_start(out=xs_table[32:96:4, :].bitcast(I32), in_=x_scales[0].bitcast(I32))
         nc.sync.dma_start(out=xw_table[:], in_=x_words[0].rearrange("p n r -> p (n r)").bitcast(I32))
         nc.sync.dma_start(out=gain[:], in_=gamma.rearrange("(p t) o -> p (t o)", t=PACK))
         nc.sync.dma_start(out=w2_codes[:], in_=w2_words[0].rearrange("p n r -> p (n r)").bitcast(I32))
@@ -61,7 +58,7 @@ def tile_picked_inorm_relu_p_kernel(
         for q in range(4):
             nc.scalar.dma_start(
                 out=xs[32 * q : 32 * q + 4, :].bitcast(I32),
-                in_=xs_picked[64 * (q // 2) + 16 * (q % 2) : 64 * (q // 2) + 16 * (q % 2) + 16 : 4, :].bitcast(I32),
+                in_=xs_picked[32 + 16 * q : 48 + 16 * q : 4, :].bitcast(I32),
             )
 
         w2_plane = keep.tile([P, N], U8, name="w2_plane", tag="picked_rows", align_bytes=64)
@@ -93,9 +90,9 @@ def tile_picked_inorm_relu_p_kernel(
             xw.append(picked)
 
         pairs = keep.tile([P, PACK, 3], F32, name="pairs")
+        nc.scalar.activation(out=pairs[:, :, 0], in_=gain[:], func=ACT.Copy, scale=float(HALF))
+        nc.scalar.activation(out=pairs[:, :, 1], in_=gain[:], func=ACT.Copy)
         minus_gain = keep.tile([P, PACK], F32, name="minus_gain")
-        nc.scalar.activation(out=pairs[:, :, 0], in_=gain[:], func=ACT.Copy)
-        nc.scalar.activation(out=pairs[:, :, 2], in_=gain[:], func=ACT.Copy, scale=float(QUARTER))
         nc.scalar.activation(out=minus_gain[:], in_=gain[:], func=ACT.Copy, scale=-1.0)
 
         idle = psum.tile([P, HALF], F32, name="idle", tag="bank7")
@@ -111,7 +108,7 @@ def tile_picked_inorm_relu_p_kernel(
             )
 
         banks = {}
-        for t, h in ((0, 0), (2, 0), (3, 0), (0, 1), (1, 0), (1, 1), (2, 1), (3, 1)):
+        for t, h in ((0, 0), (2, 0), (1, 0), (3, 0), (0, 1), (1, 1), (2, 1), (3, 1)):
             bank = psum.tile([P, HALF], F32, name=f"h{t}{h}", tag=f"bank{2 * t + h}")
             nc.tensor.matmul_mx(
                 out=bank[:],
@@ -125,130 +122,103 @@ def tile_picked_inorm_relu_p_kernel(
             banks[t, h] = bank
 
         planes = [keep.tile([P, PACK, HALF], BF16, name=f"planes{h}", align_bytes=64) for h in range(2)]
-        stats = [keep.tile([P, 12], F32, name=f"stats{t}") for t in range(PACK)]
-        scratch = keep.tile([P, 2, QUARTER], BF16, name="scratch")
-        shrunk = {t: keep.tile([P, HALF], F32, name=f"shrunk{t}") for t in (0, 1)}
+        stats = keep.tile([P, PACK, 12], F32, name="stats")
+        scratch = keep.tile([P, 2, HALF], BF16, name="scratch")
+        shrunk = [keep.tile([P, HALF], F32, name=f"shrunk{t}") for t in SCALAR_TILES]
+        moments = keep.tile([P, PACK, 2], F32, name="moments")
+        rstd = keep.tile([P, PACK], F32, name="rstd")
+        gained = {t: keep.tile([P, QUARTER], F32, name=f"gained{t}") for t in (2, 3)}
+        affine = [keep.tile([P, 3], F32, name=f"affine{t}") for t in range(PACK)]
+        nc.vector.memset(stats[:, 0:2, 3:4], float(HALF))
 
         def mean_on_scalar(t):
-            nc.vector.memset(stats[t][:, 0:6], float(QUARTER))
-            for g in range(2):
-                nc.scalar.activation(
-                    out=shrunk[t][:, QUARTER * g : QUARTER * (g + 1)], in_=banks[t, 0][:, QUARTER * g : QUARTER * (g + 1)], func=ACT.Identity,
-                    scale=1.0 / QUARTER, accum_out=stats[t][:, 3 * g + 1 : 3 * g + 2],
-                )
-
-        def spread_on_scalar(t, g):
             nc.scalar.activation(
-                out=scratch[:, g, :], in_=banks[t, 0][:, QUARTER * g : QUARTER * (g + 1)], func=ACT.Square,
-                scale=-1.0, bias=stats[t][:, 3 * g + 1 : 3 * g + 2], accum_out=stats[t][:, 3 * g + 2 : 3 * g + 3],
+                out=shrunk[t][:], in_=banks[t, 0][:], func=ACT.Identity,
+                scale=1.0 / HALF, accum_out=stats[:, t, 4:5],
             )
 
-        moments = [keep.tile([P, 2], F32, name=f"moments{t}") for t in range(PACK)]
-        rstd = [keep.tile([P, 1], F32, name=f"rstd{t}") for t in range(PACK)]
-        affine = [keep.tile([P, 3], F32, name=f"affine{t}") for t in range(PACK)]
+        def spread_on_scalar(t):
+            nc.scalar.activation(
+                out=scratch[:, t, :], in_=shrunk[t][:], func=ACT.Square,
+                scale=-float(HALF), bias=stats[:, t, 4:5], accum_out=stats[:, t, 5:6],
+            )
 
         def measure(t, h):
-            nc.vector.bn_stats(out=stats[t][:, 6 * h : 6 * (h + 1)], in_=banks[t, h][:])
+            nc.vector.bn_stats(out=stats[:, t, 6 * h : 6 * h + 6], in_=banks[t, h][:])
 
         def aggregate(t):
-            nc.vector.bn_aggr(out=moments[t][:], in_=stats[t][:])
+            nc.vector.bn_aggr(out=moments[:, t, :], in_=stats[:, t, (3 if t in SCALAR_TILES else 0) : 12])
 
-        def factors(t):
-            nc.scalar.activation(out=rstd[t][:], in_=moments[t][:, 1:2], func=ACT.Abs_reciprocal_sqrt, bias=EPS)
+        def gain_copy(t):
             nc.scalar.activation(
-                out=pairs[:, t, 1:2], in_=moments[t][:, 0:1], func=ACT.Copy, scale=minus_gain[:, t : t + 1]
+                out=gained[t][:], in_=banks[t, 0][:, 0:QUARTER], func=ACT.Copy, scale=gain[:, t : t + 1]
+            )
+
+        def roots(t):
+            nc.scalar.activation(
+                out=rstd[:, t : t + 2], in_=moments[:, t : t + 2, 1], func=ACT.Abs_reciprocal_sqrt, bias=EPS
+            )
+
+        def shift(t):
+            nc.scalar.activation(
+                out=pairs[:, t, 2:3], in_=moments[:, t, 0:1], func=ACT.Copy, scale=minus_gain[:, t : t + 1]
             )
 
         def combine(t):
-            nc.scalar.activation(out=affine[t][:], in_=pairs[:, t, :], func=ACT.Copy, scale=rstd[t][:])
+            nc.scalar.activation(out=affine[t][:], in_=pairs[:, t, :], func=ACT.Copy, scale=rstd[:, t : t + 1])
 
         def normalise(engine, t, n0, width):
             h, c0 = divmod(n0, HALF)
-            if engine == "copy":
-                nc.vector.tensor_scalar(
-                    out=planes[h][:, t, c0 : c0 + width], in0=shrunk[t][:, c0 : c0 + width],
-                    scalar1=affine[t][:, 2:3], scalar2=affine[t][:, 1:2], op0=ALU.mult, op1=ALU.add,
+            dst = planes[h][:, t, c0 : c0 + width]
+            if engine == "scalar":
+                nc.scalar.activation(
+                    out=dst, in_=banks[t, h][:, c0 : c0 + width], func=ACT.Relu,
+                    scale=affine[t][:, 1:2], bias=affine[t][:, 2:3],
                 )
             elif engine == "vector":
                 nc.vector.tensor_scalar(
-                    out=planes[h][:, t, c0 : c0 + width], in0=banks[t, h][:, c0 : c0 + width],
-                    scalar1=affine[t][:, 0:1], scalar2=affine[t][:, 1:2], op0=ALU.mult, op1=ALU.add,
+                    out=dst, in0=banks[t, h][:, c0 : c0 + width],
+                    scalar1=affine[t][:, 1:2], scalar2=affine[t][:, 2:3], op0=ALU.mult, op1=ALU.add,
+                )
+            elif engine == "gained":
+                nc.vector.tensor_scalar(
+                    out=dst, in0=gained[t][:, c0 : c0 + width],
+                    scalar1=pairs[:, t, 2:3], scalar2=rstd[:, t : t + 1], op0=ALU.add, op1=ALU.mult,
                 )
             else:
-                nc.scalar.activation(
-                    out=planes[h][:, t, c0 : c0 + width], in_=banks[t, h][:, c0 : c0 + width], func=ACT.Relu,
-                    scale=affine[t][:, 0:1], bias=affine[t][:, 1:2],
+                nc.vector.tensor_scalar(
+                    out=dst, in0=shrunk[t][:, c0 : c0 + width],
+                    scalar1=affine[t][:, 0:1], scalar2=affine[t][:, 2:3], op0=ALU.mult, op1=ALU.add,
                 )
 
-        mean_on_scalar(0)
-        measure(2, 0)
-        spread_on_scalar(0, 0)
-        spread_on_scalar(0, 1)
-        measure(3, 0)
-        measure(0, 1)
-        aggregate(0)
-        factors(0)
-        combine(0)
-        mean_on_scalar(1)
-        spread_on_scalar(1, 0)
-        spread_on_scalar(1, 1)
-        measure(1, 1)
-        measure(2, 1)
-        aggregate(1)
-        factors(1)
-        combine(1)
-        normalise("scalar", 0, 512, 256)
-        normalise("scalar", 0, 768, 256)
-        measure(3, 1)
-        aggregate(2)
-        aggregate(3)
-        factors(2)
-        factors(3)
-        combine(2)
-        combine(3)
-        normalise("copy", 0, 0, 512)
-        normalise("copy", 1, 0, 512)
-        normalise("vector", 1, 512, 512)
-        normalise("scalar", 2, 0, 128)
-        normalise("scalar", 3, 0, 128)
-        normalise("scalar", 2, 128, 128)
-        normalise("scalar", 3, 128, 128)
-        normalise("scalar", 2, 256, 256)
-        normalise("scalar", 3, 256, 256)
-        normalise("scalar", 2, 512, 256)
-        normalise("scalar", 3, 512, 256)
-        normalise("scalar", 2, 768, 256)
-        normalise("scalar", 3, 768, 256)
-
         out_view = out.rearrange("(a p) n -> p a n", p=P)
-        pieces = tuple((128 * q, 128) for q in range(8))
+        pieces = ((0, 128), (128, 128), (256, 128), (384, 128), (512, 128), (640, 128), (768, 128), (896, 128))
+        piece_bank = (0, 2, 4, 6, 1, 3, 5, 7)
         grouped = {}
+        sums = {}
 
-        def weave(engine, q, lo=0, hi=None):
+        def weave(engine, q):
             n0, width = pieces[q]
-            hi = width if hi is None else hi
             h, c0 = divmod(n0, HALF)
-            if q not in grouped:
-                grouped[q] = keep.tile([P, width, PACK], BF16, name=f"z_grouped{q}", align_bytes=64)
-            dst = grouped[q][:, lo:hi, :].rearrange("p (c i) t -> p c t i", i=4)
-            src = planes[h][:, :, c0 + lo : c0 + hi].rearrange("p t (c i) -> p c t i", i=4)
+            grouped[q] = keep.tile([P, width, PACK], BF16, name=f"z_grouped{q}", align_bytes=64)
+            dst = grouped[q][:].rearrange("p (c i) t -> p c t i", i=4)
+            src = planes[h][:, :, c0 : c0 + width].rearrange("p t (c i) -> p c t i", i=4)
             if engine == "scalar":
                 nc.scalar.activation(out=dst, in_=src, func=ACT.Relu)
             else:
                 nc.vector.tensor_scalar(out=dst, in0=src, scalar1=0.0, scalar2=None, op0=ALU.max)
 
-        def finish(q, engine):
+        def multiply(q):
             n0, width = pieces[q]
             z_codes = keep.tile([P, width], U32, name=f"z_codes{q}", align_bytes=64)
             z_plane = keep.tile([P, width], U8, name=f"z_plane{q}", align_bytes=64)
             nc.vector.quantize_mx(
                 out=z_codes[:].bitcast(FP8X4), scales=z_plane[:], in_=grouped[q][:].rearrange("p n t -> p (n t)")
             )
-            result = keep.tile([P, 2, width], F32, name=f"result{q}")
-            acc = psum.tile([P, 2, width], F32, name=f"acc{q}", tag=f"bank{(0, 2, 1, 3, 4, 6, 7, 5)[q]}")
+            sums[q] = psum.tile([P, 2, width], F32, name=f"acc{q}", tag=f"bank{piece_bank[q]}")
             for a in range(2):
                 nc.tensor.matmul_mx(
-                    out=acc[:, a, :],
+                    out=sums[q][:, a, :],
                     lhsT=w2_codes[:, P * a : P * (a + 1)].bitcast(FP8X4),
                     lhsT_scale=w2_plane[:, P * a : P * (a + 1)],
                     rhs=z_codes[:].bitcast(FP8X4),
@@ -256,25 +226,78 @@ def tile_picked_inorm_relu_p_kernel(
                     start=True,
                     stop=True,
                 )
+
+        def store(engine, q):
+            n0, width = pieces[q]
+            result = keep.tile([P, 2, width], F32, name=f"result{q}")
             if engine == "vector":
-                nc.vector.tensor_copy(out=result[:], in_=acc[:])
+                nc.vector.tensor_copy(out=result[:], in_=sums[q][:])
             else:
-                nc.scalar.copy(out=result[:], in_=acc[:])
+                nc.scalar.copy(out=result[:], in_=sums[q][:])
             nc.sync.dma_start(out=out_view[:, :, n0 : n0 + width], in_=result[:])
+
+        mean_on_scalar(0)
+        mean_on_scalar(1)
+        measure(2, 0)
+        spread_on_scalar(0)
+        measure(3, 0)
+        measure(0, 1)
+        spread_on_scalar(1)
+        gain_copy(2)
+        gain_copy(3)
+        measure(1, 1)
+        aggregate(0)
+        measure(2, 1)
+        aggregate(1)
+        shift(0)
+        roots(0)
+        shift(1)
+        measure(3, 1)
+        aggregate(2)
+        aggregate(3)
+        combine(0)
+        combine(1)
+        shift(2)
+        roots(2)
+        shift(3)
+        normalise("copy", 0, 0, 512)
+        normalise("copy", 1, 0, 512)
+        normalise("gained", 2, 0, 256)
+        normalise("gained", 3, 0, 256)
+        combine(2)
+        combine(3)
+        normalise("scalar", 2, 256, 256)
+        normalise("scalar", 3, 256, 256)
 
         weave("vector", 0)
         weave("vector", 1)
-        finish(0, "scalar")
+        multiply(0)
+        normalise("scalar", 0, 512, 256)
+        normalise("scalar", 1, 512, 256)
+        normalise("scalar", 2, 512, 256)
+        normalise("scalar", 3, 512, 256)
         weave("vector", 2)
-        finish(1, "scalar")
-        weave("scalar", 7)
+        multiply(1)
+        store("scalar", 0)
         weave("vector", 3)
-        finish(2, "scalar")
+        multiply(2)
+        store("scalar", 1)
+        normalise("scalar", 0, 768, 256)
+        normalise("scalar", 1, 768, 256)
+        normalise("scalar", 2, 768, 256)
+        normalise("scalar", 3, 768, 256)
         weave("vector", 4)
-        finish(3, "scalar")
+        multiply(3)
+        store("scalar", 2)
         weave("vector", 5)
-        finish(4, "scalar")
+        multiply(4)
+        store("scalar", 3)
         weave("vector", 6)
-        finish(5, "vector")
-        finish(7, "scalar")
-        finish(6, "vector")
+        multiply(5)
+        weave("vector", 7)
+        store("scalar", 4)
+        multiply(6)
+        store("scalar", 5)
+        multiply(7)
+        store("scalar", 6)
+        store("vector", 7)

@@ -96,7 +96,7 @@ def tile_picked_inorm_relu_p_kernel(
         nc.scalar.activation(out=minus_gain[:], in_=gain[:], func=ACT.Copy, scale=-1.0)
 
         idle = psum.tile([P, HALF], F32, name="idle", tag="bank7")
-        for turn in range(2):
+        for turn in range(3):
             nc.tensor.matmul_mx(
                 out=idle[:],
                 lhsT=w1_codes[:, 0:P].bitcast(FP8X4),
@@ -110,15 +110,16 @@ def tile_picked_inorm_relu_p_kernel(
         banks = {}
         for t, h in ((0, 0), (2, 0), (1, 0), (3, 0), (0, 1), (1, 1), (2, 1), (3, 1)):
             bank = psum.tile([P, HALF], F32, name=f"h{t}{h}", tag=f"bank{2 * t + h}")
-            nc.tensor.matmul_mx(
-                out=bank[:],
-                lhsT=w1_codes[:, P * t : P * (t + 1)].bitcast(FP8X4),
-                lhsT_scale=w1_plane[:, P * t : P * (t + 1)],
-                rhs=xw[h][:].bitcast(FP8X4),
-                rhs_scale=xs[:, HALF * h : HALF * (h + 1)],
-                start=True,
-                stop=True,
-            )
+            for c0 in (0, QUARTER):
+                nc.tensor.matmul_mx(
+                    out=bank[:, c0 : c0 + QUARTER],
+                    lhsT=w1_codes[:, P * t : P * (t + 1)].bitcast(FP8X4),
+                    lhsT_scale=w1_plane[:, P * t : P * (t + 1)],
+                    rhs=xw[h][:, c0 : c0 + QUARTER].bitcast(FP8X4),
+                    rhs_scale=xs[:, HALF * h + c0 : HALF * h + c0 + QUARTER],
+                    start=True,
+                    stop=True,
+                )
             banks[t, h] = bank
 
         planes = [keep.tile([P, PACK, HALF], BF16, name=f"planes{h}", align_bytes=64) for h in range(2)]
@@ -244,18 +245,18 @@ def tile_picked_inorm_relu_p_kernel(
         measure(0, 1)
         spread_on_scalar(1)
         gain_copy(2)
-        gain_copy(3)
         measure(1, 1)
         aggregate(0)
         measure(2, 1)
         aggregate(1)
+        gain_copy(3)
         shift(0)
         roots(0)
         shift(1)
+        combine(0)
         measure(3, 1)
         aggregate(2)
         aggregate(3)
-        combine(0)
         combine(1)
         shift(2)
         roots(2)
@@ -271,8 +272,12 @@ def tile_picked_inorm_relu_p_kernel(
 
         weave("vector", 0)
         weave("vector", 1)
+        normalise("vector", 1, 768, 256)
         multiply(0)
-        normalise("scalar", 0, 512, 256)
+        normalise("scalar", 0, 512, 128)
+        normalise("scalar", 0, 640, 128)
+        normalise("scalar", 0, 768, 128)
+        normalise("scalar", 0, 896, 128)
         normalise("scalar", 1, 512, 256)
         normalise("scalar", 2, 512, 256)
         normalise("scalar", 3, 512, 256)
@@ -282,8 +287,6 @@ def tile_picked_inorm_relu_p_kernel(
         weave("vector", 3)
         multiply(2)
         store("scalar", 1)
-        normalise("scalar", 0, 768, 256)
-        normalise("scalar", 1, 768, 256)
         normalise("scalar", 2, 768, 256)
         normalise("scalar", 3, 768, 256)
         weave("vector", 4)

@@ -237,6 +237,34 @@ def tile_picked_inorm_relu_p_kernel(
                 nc.scalar.copy(out=result[:], in_=sums[q][:])
             nc.sync.dma_start(out=out_view[:, :, n0 : n0 + width], in_=result[:])
 
+        def multiply_split(q, *two_banks):
+            n0, width = pieces[q]
+            z_codes = keep.tile([P, width], U32, name=f"z_codes{q}", align_bytes=64)
+            z_plane = keep.tile([P, width], U8, name=f"z_plane{q}", align_bytes=64)
+            nc.vector.quantize_mx(
+                out=z_codes[:].bitcast(FP8X4), scales=z_plane[:], in_=grouped[q][:].rearrange("p n t -> p (n t)")
+            )
+            for a in range(2):
+                sums[q, a] = psum.tile([P, width], F32, name=f"acc{q}{a}", tag=f"bank{two_banks[a]}")
+                nc.tensor.matmul_mx(
+                    out=sums[q, a][:],
+                    lhsT=w2_codes[:, P * a : P * (a + 1)].bitcast(FP8X4),
+                    lhsT_scale=w2_plane[:, P * a : P * (a + 1)],
+                    rhs=z_codes[:].bitcast(FP8X4),
+                    rhs_scale=z_plane[:],
+                    start=True,
+                    stop=True,
+                )
+
+        def store_half(engine, q, a):
+            n0, width = pieces[q]
+            result = keep.tile([P, width], F32, name=f"result{q}{a}")
+            if engine == "vector":
+                nc.vector.tensor_copy(out=result[:], in_=sums[q, a][:])
+            else:
+                nc.scalar.copy(out=result[:], in_=sums[q, a][:])
+            nc.sync.dma_start(out=out_view[:, a, n0 : n0 + width], in_=result[:])
+
         mean_on_scalar(0)
         mean_on_scalar(1)
         measure(2, 0)
@@ -299,8 +327,10 @@ def tile_picked_inorm_relu_p_kernel(
         multiply(5)
         weave("vector", 7)
         store("scalar", 4)
-        multiply(6)
+        multiply_split(6, 5, 0)
         store("scalar", 5)
-        multiply(7)
-        store("scalar", 6)
-        store("vector", 7)
+        multiply_split(7, 7, 2)
+        store_half("scalar", 6, 0)
+        store_half("vector", 6, 1)
+        store_half("scalar", 7, 0)
+        store_half("vector", 7, 1)

@@ -20,7 +20,7 @@ P = 128
 PACK = 4
 HALF = 512
 QUARTER = 256
-SCALAR_TILES = (0, 1)
+KEPT = {0: 512, 1: 512, 2: 256}
 
 
 def tile_picked_inorm_relu_p_kernel(
@@ -90,7 +90,8 @@ def tile_picked_inorm_relu_p_kernel(
             xw.append(picked)
 
         pairs = keep.tile([P, PACK, 3], F32, name="pairs")
-        nc.scalar.activation(out=pairs[:, :, 0], in_=gain[:], func=ACT.Copy, scale=float(HALF))
+        for t, width in KEPT.items():
+            nc.scalar.activation(out=pairs[:, t, 0:1], in_=gain[:, t : t + 1], func=ACT.Copy, scale=float(width))
         nc.scalar.activation(out=pairs[:, :, 1], in_=gain[:], func=ACT.Copy)
         minus_gain = keep.tile([P, PACK], F32, name="minus_gain")
         nc.scalar.activation(out=minus_gain[:], in_=gain[:], func=ACT.Copy, scale=-1.0)
@@ -108,7 +109,7 @@ def tile_picked_inorm_relu_p_kernel(
             )
 
         banks = {}
-        for t, h in ((0, 0), (2, 0), (1, 0), (3, 0), (0, 1), (1, 1), (2, 1), (3, 1)):
+        for t, h in ((0, 0), (3, 0), (1, 0), (2, 0), (0, 1), (1, 1), (2, 1), (3, 1)):
             bank = psum.tile([P, HALF], F32, name=f"h{t}{h}", tag=f"bank{2 * t + h}")
             for c0 in (0, QUARTER):
                 nc.tensor.matmul_mx(
@@ -123,41 +124,50 @@ def tile_picked_inorm_relu_p_kernel(
             banks[t, h] = bank
 
         planes = [keep.tile([P, PACK, HALF], BF16, name=f"planes{h}", align_bytes=64) for h in range(2)]
-        stats = keep.tile([P, PACK, 12], F32, name="stats")
-        scratch = keep.tile([P, 2, HALF], BF16, name="scratch")
-        shrunk = [keep.tile([P, HALF], F32, name=f"shrunk{t}") for t in SCALAR_TILES]
+        stats = keep.tile([P, PACK, 24], F32, name="stats")
+        scratch = keep.tile([P, PACK, HALF], BF16, name="scratch")
+        shrunk = {t: keep.tile([P, width], F32, name=f"shrunk{t}") for t, width in KEPT.items()}
         moments = keep.tile([P, PACK, 2], F32, name="moments")
         rstd = keep.tile([P, PACK], F32, name="rstd")
         gained = {t: keep.tile([P, QUARTER], F32, name=f"gained{t}") for t in (2, 3)}
         affine = [keep.tile([P, 3], F32, name=f"affine{t}") for t in range(PACK)]
-        nc.vector.memset(stats[:, 0:2, 3:4], float(HALF))
+        for t, width in KEPT.items():
+            nc.vector.memset(stats[:, t, 6:7], float(width))
 
         def mean_on_scalar(t):
             nc.scalar.activation(
-                out=shrunk[t][:], in_=banks[t, 0][:], func=ACT.Identity,
-                scale=1.0 / HALF, accum_out=stats[:, t, 4:5],
+                out=shrunk[t][:], in_=banks[t, 0][:, 0 : KEPT[t]], func=ACT.Identity,
+                scale=1.0 / KEPT[t], accum_out=stats[:, t, 7:8],
             )
 
         def spread_on_scalar(t):
             nc.scalar.activation(
-                out=scratch[:, t, :], in_=shrunk[t][:], func=ACT.Square,
-                scale=-float(HALF), bias=stats[:, t, 4:5], accum_out=stats[:, t, 5:6],
+                out=scratch[:, t, 0 : KEPT[t]], in_=shrunk[t][:], func=ACT.Square,
+                scale=-float(KEPT[t]), bias=stats[:, t, 7:8], accum_out=stats[:, t, 8:9],
             )
 
         def measure(t, h):
-            nc.vector.bn_stats(out=stats[:, t, 6 * h : 6 * h + 6], in_=banks[t, h][:])
+            first = 9 if h else (0 if t in KEPT else 3)
+            c0 = 0 if h else KEPT.get(t, 0)
+            nc.vector.bn_stats(out=stats[:, t, first : first + 6], in_=banks[t, h][:, c0:HALF])
+
+        def measure_last(part):
+            nc.vector.bn_stats(
+                out=stats[:, 3, 9 + 6 * part : 15 + 6 * part], in_=banks[3, 1][:, QUARTER * part : QUARTER * (part + 1)]
+            )
 
         def aggregate(t):
-            nc.vector.bn_aggr(out=moments[:, t, :], in_=stats[:, t, (3 if t in SCALAR_TILES else 0) : 12])
+            first = {0: 3, HALF: 6}.get(KEPT.get(t, 0), 0)
+            nc.vector.bn_aggr(out=moments[:, t, :], in_=stats[:, t, first : (21 if t == 3 else 15)])
 
         def gain_copy(t):
             nc.scalar.activation(
                 out=gained[t][:], in_=banks[t, 0][:, 0:QUARTER], func=ACT.Copy, scale=gain[:, t : t + 1]
             )
 
-        def roots(t):
+        def roots(t, count=2):
             nc.scalar.activation(
-                out=rstd[:, t : t + 2], in_=moments[:, t : t + 2, 1], func=ACT.Abs_reciprocal_sqrt, bias=EPS
+                out=rstd[:, t : t + count], in_=moments[:, t : t + count, 1], func=ACT.Abs_reciprocal_sqrt, bias=EPS
             )
 
         def shift(t):
@@ -166,7 +176,10 @@ def tile_picked_inorm_relu_p_kernel(
             )
 
         def combine(t):
-            nc.scalar.activation(out=affine[t][:], in_=pairs[:, t, :], func=ACT.Copy, scale=rstd[:, t : t + 1])
+            first = 0 if t in KEPT else 1
+            nc.scalar.activation(
+                out=affine[t][:, first:3], in_=pairs[:, t, first:3], func=ACT.Copy, scale=rstd[:, t : t + 1]
+            )
 
         def normalise(engine, t, n0, width):
             h, c0 = divmod(n0, HALF)
@@ -198,12 +211,14 @@ def tile_picked_inorm_relu_p_kernel(
         grouped = {}
         sums = {}
 
-        def weave(engine, q):
+        def weave(engine, q, first_point=0, count=None):
             n0, width = pieces[q]
-            h, c0 = divmod(n0, HALF)
-            grouped[q] = keep.tile([P, width, PACK], BF16, name=f"z_grouped{q}", align_bytes=64)
-            dst = grouped[q][:].rearrange("p (c i) t -> p c t i", i=4)
-            src = planes[h][:, :, c0 : c0 + width].rearrange("p t (c i) -> p c t i", i=4)
+            if q not in grouped:
+                grouped[q] = keep.tile([P, width, PACK], BF16, name=f"z_grouped{q}", align_bytes=64)
+            count = count or width
+            h, c0 = divmod(n0 + first_point, HALF)
+            dst = grouped[q][:, first_point : first_point + count].rearrange("p (c i) t -> p c t i", i=4)
+            src = planes[h][:, :, c0 : c0 + count].rearrange("p t (c i) -> p c t i", i=4)
             if engine == "scalar":
                 nc.scalar.activation(out=dst, in_=src, func=ACT.Relu)
             else:
@@ -267,68 +282,75 @@ def tile_picked_inorm_relu_p_kernel(
 
         mean_on_scalar(0)
         mean_on_scalar(1)
+        measure(3, 0)
         measure(2, 0)
         spread_on_scalar(0)
-        measure(3, 0)
+        mean_on_scalar(2)
         measure(0, 1)
         spread_on_scalar(1)
-        gain_copy(2)
         measure(1, 1)
         aggregate(0)
+        spread_on_scalar(2)
         measure(2, 1)
         aggregate(1)
-        gain_copy(3)
-        shift(0)
-        roots(0)
-        shift(1)
-        combine(0)
-        measure(3, 1)
         aggregate(2)
+        measure_last(0)
+        measure_last(1)
         aggregate(3)
-        combine(1)
-        shift(2)
-        roots(2)
+        roots(3, 1)
         shift(3)
-        normalise("copy", 0, 0, 512)
-        normalise("copy", 1, 0, 512)
-        normalise("gained", 2, 0, 256)
-        normalise("gained", 3, 0, 256)
+        roots(2, 1)
+        shift(2)
         combine(2)
+        roots(0, 1)
+        shift(0)
+        combine(0)
+        roots(1, 1)
+        shift(1)
+        combine(1)
+        gain_copy(3)
+        normalise("gained", 3, 0, 128)
+        normalise("copy", 2, 0, 256)
+        normalise("copy", 0, 0, 256)
+        normalise("copy", 1, 0, 256)
+        normalise("gained", 3, 128, 128)
         combine(3)
-        normalise("scalar", 2, 256, 256)
-        normalise("scalar", 3, 256, 256)
-
         weave("vector", 0)
         weave("vector", 1)
-        normalise("vector", 1, 768, 256)
         multiply(0)
-        normalise("scalar", 0, 512, 128)
-        normalise("scalar", 0, 640, 128)
-        normalise("scalar", 0, 768, 128)
-        normalise("scalar", 0, 896, 128)
-        normalise("scalar", 1, 512, 256)
-        normalise("scalar", 2, 512, 256)
-        normalise("scalar", 3, 512, 256)
+        store("scalar", 0)
+        normalise("copy", 0, 256, 256)
+        normalise("copy", 1, 256, 256)
+        normalise("scalar", 2, 256, 256)
+        normalise("scalar", 3, 256, 256)
         weave("vector", 2)
         multiply(1)
-        store("scalar", 0)
+        store("scalar", 1)
+        normalise("scalar", 0, 512, 128)
+        normalise("scalar", 0, 640, 128)
+        normalise("scalar", 1, 512, 128)
+        normalise("scalar", 1, 640, 128)
+        normalise("scalar", 2, 512, 256)
+        normalise("scalar", 3, 512, 256)
         weave("vector", 3)
         multiply(2)
-        store("scalar", 1)
+        store("scalar", 2)
+        normalise("scalar", 0, 768, 128)
+        normalise("scalar", 0, 896, 128)
+        normalise("scalar", 1, 768, 256)
         normalise("scalar", 2, 768, 256)
         normalise("scalar", 3, 768, 256)
         weave("vector", 4)
         multiply(3)
-        store("scalar", 2)
+        store("scalar", 3)
         weave("vector", 5)
         multiply(4)
-        store("scalar", 3)
+        store("scalar", 4)
         weave("vector", 6)
         multiply(5)
-        weave("vector", 7)
-        store("scalar", 4)
-        multiply_split(6, 5, 0)
         store("scalar", 5)
+        weave("vector", 7)
+        multiply_split(6, 5, 0)
         multiply_split(7, 7, 2)
         store_half("scalar", 6, 0)
         store_half("vector", 6, 1)

@@ -42,6 +42,9 @@ def tile_picked_inorm_relu_p_kernel(
         nc.vector.memset(xs_table[:].bitcast(I32), 0)
         nc.vector.memset(xs[:].bitcast(I32), 0)
 
+        w2_plane = keep.tile([P, N], U8, name="w2_plane", align_bytes=64)
+        nc.vector.memset(w2_plane[:].bitcast(I32), 0)
+
         warm = keep.tile([P, 2], F32, name="warm")
         nc.vector.memset(warm[:, 0:1], 1.0)
         nc.scalar.activation(out=warm[:, 1:2], in_=warm[:, 0:1], func=ACT.Abs_reciprocal_sqrt, bias=EPS)
@@ -53,7 +56,7 @@ def tile_picked_inorm_relu_p_kernel(
         nc.sync.dma_start(out=gain[:], in_=gamma.rearrange("(p t) o -> p (t o)", t=PACK))
         nc.sync.dma_start(out=w2_codes[:], in_=w2_words[0].rearrange("p n r -> p (n r)").bitcast(I32))
 
-        xs_picked = keep.tile([P, S], U8, name="xs_picked", tag="picked_rows", align_bytes=64)
+        xs_picked = keep.tile([P, S], U8, name="xs_picked", align_bytes=64)
         nc.vector.tensor_copy(out=xs_picked[:], in_=xs_table[:].indirect(offsets[:]))
         for q in range(4):
             nc.scalar.dma_start(
@@ -61,8 +64,6 @@ def tile_picked_inorm_relu_p_kernel(
                 in_=xs_picked[32 + 16 * q : 48 + 16 * q : 4, :].bitcast(I32),
             )
 
-        w2_plane = keep.tile([P, N], U8, name="w2_plane", tag="picked_rows", align_bytes=64)
-        nc.vector.memset(w2_plane[:].bitcast(I32), 0)
         for q in range(4):
             nc.sync.dma_start(
                 out=w2_plane[32 * q : 32 * q + 4, :].bitcast(I32),

@@ -218,8 +218,8 @@ def tile_picked_inorm_relu_p_kernel(
                 grouped[q] = keep.tile([P, width, PACK], BF16, name=f"z_grouped{q}", align_bytes=64)
             count = count or width
             h, c0 = divmod(n0 + first_point, HALF)
-            dst = grouped[q][:, first_point : first_point + count].rearrange("p (c i) t -> p c t i", i=4)
-            src = planes[h][:, :, c0 : c0 + count].rearrange("p t (c i) -> p c t i", i=4)
+            dst = grouped[q][:, first_point : first_point + count].rearrange("p (c i) t -> p c t i", i=8)
+            src = planes[h][:, :, c0 : c0 + count].rearrange("p t (c i) -> p c t i", i=8)
             if engine == "scalar":
                 nc.scalar.activation(out=dst, in_=src, func=ACT.Relu)
             else:

@@ -20,7 +20,15 @@ P = 128
 PACK = 4
 HALF = 512
 QUARTER = 256
-KEPT = {0: 512, 1: 512, 2: 256}
+PIECE = 128
+PIECES = S // PIECE
+LINE = 8
+LAST = PACK - 1
+KEPT = {0: HALF, 1: HALF, 2: QUARTER}
+BESIDE_KEPT, UNKEPT, SCALAR_TRIPLE, SECOND_HALF = 0, 3, 6, 9
+TWO_TRIPLES = 6
+PIECE_BANK = (0, 2, 4, 6, 1, 3)
+SPLIT_BANKS = {6: (5, 0), 7: (7, 2)}
 
 
 def tile_picked_inorm_relu_p_kernel(
@@ -90,10 +98,10 @@ def tile_picked_inorm_relu_p_kernel(
             )
             xw.append(picked)
 
-        pairs = keep.tile([P, PACK, 3], F32, name="pairs")
+        factors = keep.tile([P, PACK, 3], F32, name="factors")
         for t, width in KEPT.items():
-            nc.scalar.activation(out=pairs[:, t, 0:1], in_=gain[:, t : t + 1], func=ACT.Copy, scale=float(width))
-        nc.scalar.activation(out=pairs[:, :, 1], in_=gain[:], func=ACT.Copy)
+            nc.scalar.activation(out=factors[:, t, 0:1], in_=gain[:, t : t + 1], func=ACT.Copy, scale=float(width))
+        nc.scalar.activation(out=factors[:, :, 1], in_=gain[:], func=ACT.Copy)
         minus_gain = keep.tile([P, PACK], F32, name="minus_gain")
         nc.scalar.activation(out=minus_gain[:], in_=gain[:], func=ACT.Copy, scale=-1.0)
 
@@ -124,118 +132,99 @@ def tile_picked_inorm_relu_p_kernel(
                 )
             banks[t, h] = bank
 
-        planes = [keep.tile([P, PACK, HALF], BF16, name=f"planes{h}", align_bytes=64) for h in range(2)]
+        z_rows = [keep.tile([P, PACK, HALF], BF16, name=f"z_rows{h}", align_bytes=64) for h in range(2)]
         stats = keep.tile([P, PACK, 24], F32, name="stats")
-        scratch = keep.tile([P, PACK, HALF], BF16, name="scratch")
+        squares = keep.tile([P, PACK, HALF], BF16, name="squares")
         shrunk = {t: keep.tile([P, width], F32, name=f"shrunk{t}") for t, width in KEPT.items()}
         moments = keep.tile([P, PACK, 2], F32, name="moments")
         rstd = keep.tile([P, PACK], F32, name="rstd")
-        gained = {t: keep.tile([P, QUARTER], F32, name=f"gained{t}") for t in (2, 3)}
+        gained = keep.tile([P, QUARTER], F32, name="gained")
         affine = [keep.tile([P, 3], F32, name=f"affine{t}") for t in range(PACK)]
         for t, width in KEPT.items():
-            nc.vector.memset(stats[:, t, 6:7], float(width))
+            nc.vector.memset(stats[:, t, SCALAR_TRIPLE : SCALAR_TRIPLE + 1], float(width))
 
         def mean_on_scalar(t):
             nc.scalar.activation(
                 out=shrunk[t][:], in_=banks[t, 0][:, 0 : KEPT[t]], func=ACT.Identity,
-                scale=1.0 / KEPT[t], accum_out=stats[:, t, 7:8],
+                scale=1.0 / KEPT[t], accum_out=stats[:, t, SCALAR_TRIPLE + 1 : SCALAR_TRIPLE + 2],
             )
 
         def spread_on_scalar(t):
             nc.scalar.activation(
-                out=scratch[:, t, 0 : KEPT[t]], in_=shrunk[t][:], func=ACT.Square,
-                scale=-float(KEPT[t]), bias=stats[:, t, 7:8], accum_out=stats[:, t, 8:9],
+                out=squares[:, t, 0 : KEPT[t]], in_=shrunk[t][:], func=ACT.Square,
+                scale=-float(KEPT[t]), bias=stats[:, t, SCALAR_TRIPLE + 1 : SCALAR_TRIPLE + 2],
+                accum_out=stats[:, t, SCALAR_TRIPLE + 2 : SCALAR_TRIPLE + 3],
             )
 
-        def measure(t, h):
-            first = 9 if h else (0 if t in KEPT else 3)
-            c0 = 0 if h else KEPT.get(t, 0)
-            nc.vector.bn_stats(out=stats[:, t, first : first + 6], in_=banks[t, h][:, c0:HALF])
+        def measure(t, h, c0, c1, column):
+            nc.vector.bn_stats(out=stats[:, t, column : column + TWO_TRIPLES], in_=banks[t, h][:, c0:c1])
 
-        def measure_last(part):
-            nc.vector.bn_stats(
-                out=stats[:, 3, 9 + 6 * part : 15 + 6 * part], in_=banks[3, 1][:, QUARTER * part : QUARTER * (part + 1)]
-            )
+        def aggregate(t, first, last):
+            nc.vector.bn_aggr(out=moments[:, t, :], in_=stats[:, t, first:last])
 
-        def aggregate(t):
-            first = {0: 3, HALF: 6}.get(KEPT.get(t, 0), 0)
-            nc.vector.bn_aggr(out=moments[:, t, :], in_=stats[:, t, first : (21 if t == 3 else 15)])
-
-        def gain_copy(t):
+        def root(t):
             nc.scalar.activation(
-                out=gained[t][:], in_=banks[t, 0][:, 0:QUARTER], func=ACT.Copy, scale=gain[:, t : t + 1]
-            )
-
-        def roots(t, count=2):
-            nc.scalar.activation(
-                out=rstd[:, t : t + count], in_=moments[:, t : t + count, 1], func=ACT.Abs_reciprocal_sqrt, bias=EPS
+                out=rstd[:, t : t + 1], in_=moments[:, t : t + 1, 1], func=ACT.Abs_reciprocal_sqrt, bias=EPS
             )
 
         def shift(t):
             nc.scalar.activation(
-                out=pairs[:, t, 2:3], in_=moments[:, t, 0:1], func=ACT.Copy, scale=minus_gain[:, t : t + 1]
+                out=factors[:, t, 2:3], in_=moments[:, t, 0:1], func=ACT.Copy, scale=minus_gain[:, t : t + 1]
             )
 
         def combine(t):
             first = 0 if t in KEPT else 1
             nc.scalar.activation(
-                out=affine[t][:, first:3], in_=pairs[:, t, first:3], func=ACT.Copy, scale=rstd[:, t : t + 1]
+                out=affine[t][:, first:3], in_=factors[:, t, first:3], func=ACT.Copy, scale=rstd[:, t : t + 1]
             )
 
-        def normalise(engine, t, n0, width):
+        def z_slice(t, n0, width):
             h, c0 = divmod(n0, HALF)
-            dst = planes[h][:, t, c0 : c0 + width]
-            if engine == "scalar":
-                nc.scalar.activation(
-                    out=dst, in_=banks[t, h][:, c0 : c0 + width], func=ACT.Relu,
-                    scale=affine[t][:, 1:2], bias=affine[t][:, 2:3],
-                )
-            elif engine == "vector":
-                nc.vector.tensor_scalar(
-                    out=dst, in0=banks[t, h][:, c0 : c0 + width],
-                    scalar1=affine[t][:, 1:2], scalar2=affine[t][:, 2:3], op0=ALU.mult, op1=ALU.add,
-                )
-            elif engine == "gained":
-                nc.vector.tensor_scalar(
-                    out=dst, in0=gained[t][:, c0 : c0 + width],
-                    scalar1=pairs[:, t, 2:3], scalar2=rstd[:, t : t + 1], op0=ALU.add, op1=ALU.mult,
-                )
-            else:
-                nc.vector.tensor_scalar(
-                    out=dst, in0=shrunk[t][:, c0 : c0 + width],
-                    scalar1=affine[t][:, 0:1], scalar2=affine[t][:, 2:3], op0=ALU.mult, op1=ALU.add,
-                )
+            return z_rows[h][:, t, c0 : c0 + width]
+
+        def normalise_bank(t, n0, width):
+            h, c0 = divmod(n0, HALF)
+            nc.scalar.activation(
+                out=z_slice(t, n0, width), in_=banks[t, h][:, c0 : c0 + width], func=ACT.Relu,
+                scale=affine[t][:, 1:2], bias=affine[t][:, 2:3],
+            )
+
+        def normalise_kept(t, n0, width):
+            nc.vector.tensor_scalar(
+                out=z_slice(t, n0, width), in0=shrunk[t][:, n0 : n0 + width],
+                scalar1=affine[t][:, 0:1], scalar2=affine[t][:, 2:3], op0=ALU.mult, op1=ALU.add,
+            )
+
+        def normalise_gained(n0, width):
+            nc.vector.tensor_scalar(
+                out=z_slice(LAST, n0, width), in0=gained[:, n0 : n0 + width],
+                scalar1=factors[:, LAST, 2:3], scalar2=rstd[:, LAST : LAST + 1], op0=ALU.add, op1=ALU.mult,
+            )
 
         out_view = out.rearrange("(a p) n -> p a n", p=P)
-        pieces = ((0, 128), (128, 128), (256, 128), (384, 128), (512, 128), (640, 128), (768, 128), (896, 128))
-        piece_bank = (0, 2, 4, 6, 1, 3, 5, 7)
         grouped = {}
         sums = {}
 
-        def weave(engine, q, first_point=0, count=None):
-            n0, width = pieces[q]
-            if q not in grouped:
-                grouped[q] = keep.tile([P, width, PACK], BF16, name=f"z_grouped{q}", align_bytes=64)
-            count = count or width
-            h, c0 = divmod(n0 + first_point, HALF)
-            dst = grouped[q][:, first_point : first_point + count].rearrange("p (c i) t -> p c t i", i=8)
-            src = planes[h][:, :, c0 : c0 + count].rearrange("p t (c i) -> p c t i", i=8)
-            if engine == "scalar":
-                nc.scalar.activation(out=dst, in_=src, func=ACT.Relu)
-            else:
-                nc.vector.tensor_scalar(out=dst, in0=src, scalar1=0.0, scalar2=None, op0=ALU.max)
+        def interleave(q):
+            h, c0 = divmod(PIECE * q, HALF)
+            grouped[q] = keep.tile([P, PIECE, PACK], BF16, name=f"z_grouped{q}", align_bytes=64)
+            dst = grouped[q][:].rearrange("p (c i) t -> p c t i", i=LINE)
+            src = z_rows[h][:, :, c0 : c0 + PIECE].rearrange("p t (c i) -> p c t i", i=LINE)
+            nc.vector.tensor_scalar(out=dst, in0=src, scalar1=0.0, scalar2=None, op0=ALU.max)
 
         def multiply(q):
-            n0, width = pieces[q]
-            z_codes = keep.tile([P, width], U32, name=f"z_codes{q}", align_bytes=64)
-            z_plane = keep.tile([P, width], U8, name=f"z_plane{q}", align_bytes=64)
+            z_codes = keep.tile([P, PIECE], U32, name=f"z_codes{q}", align_bytes=64)
+            z_plane = keep.tile([P, PIECE], U8, name=f"z_plane{q}", align_bytes=64)
             nc.vector.quantize_mx(
                 out=z_codes[:].bitcast(FP8X4), scales=z_plane[:], in_=grouped[q][:].rearrange("p n t -> p (n t)")
             )
-            sums[q] = psum.tile([P, 2, width], F32, name=f"acc{q}", tag=f"bank{piece_bank[q]}")
+            if q not in SPLIT_BANKS:
+                sums[q] = psum.tile([P, 2, PIECE], F32, name=f"acc{q}", tag=f"bank{PIECE_BANK[q]}")
             for a in range(2):
+                if q in SPLIT_BANKS:
+                    sums[q, a] = psum.tile([P, PIECE], F32, name=f"acc{q}{a}", tag=f"bank{SPLIT_BANKS[q][a]}")
                 nc.tensor.matmul_mx(
-                    out=sums[q][:, a, :],
+                    out=sums[q, a][:] if q in SPLIT_BANKS else sums[q][:, a, :],
                     lhsT=w2_codes[:, P * a : P * (a + 1)].bitcast(FP8X4),
                     lhsT_scale=w2_plane[:, P * a : P * (a + 1)],
                     rhs=z_codes[:].bitcast(FP8X4),
@@ -244,116 +233,78 @@ def tile_picked_inorm_relu_p_kernel(
                     stop=True,
                 )
 
-        def store(engine, q):
-            n0, width = pieces[q]
-            result = keep.tile([P, 2, width], F32, name=f"result{q}")
-            if engine == "vector":
-                nc.vector.tensor_copy(out=result[:], in_=sums[q][:])
-            else:
-                nc.scalar.copy(out=result[:], in_=sums[q][:])
-            nc.sync.dma_start(out=out_view[:, :, n0 : n0 + width], in_=result[:])
+        def store(q):
+            result = keep.tile([P, 2, PIECE], F32, name=f"result{q}")
+            nc.scalar.copy(out=result[:], in_=sums[q][:])
+            nc.sync.dma_start(out=out_view[:, :, PIECE * q : PIECE * (q + 1)], in_=result[:])
 
-        def multiply_split(q, *two_banks):
-            n0, width = pieces[q]
-            z_codes = keep.tile([P, width], U32, name=f"z_codes{q}", align_bytes=64)
-            z_plane = keep.tile([P, width], U8, name=f"z_plane{q}", align_bytes=64)
-            nc.vector.quantize_mx(
-                out=z_codes[:].bitcast(FP8X4), scales=z_plane[:], in_=grouped[q][:].rearrange("p n t -> p (n t)")
-            )
-            for a in range(2):
-                sums[q, a] = psum.tile([P, width], F32, name=f"acc{q}{a}", tag=f"bank{two_banks[a]}")
-                nc.tensor.matmul_mx(
-                    out=sums[q, a][:],
-                    lhsT=w2_codes[:, P * a : P * (a + 1)].bitcast(FP8X4),
-                    lhsT_scale=w2_plane[:, P * a : P * (a + 1)],
-                    rhs=z_codes[:].bitcast(FP8X4),
-                    rhs_scale=z_plane[:],
-                    start=True,
-                    stop=True,
-                )
+        def store_halves(q):
+            for a, copy in enumerate((nc.scalar.copy, nc.vector.tensor_copy)):
+                result = keep.tile([P, PIECE], F32, name=f"result{q}{a}")
+                copy(out=result[:], in_=sums[q, a][:])
+                nc.sync.dma_start(out=out_view[:, a, PIECE * q : PIECE * (q + 1)], in_=result[:])
 
-        def store_half(engine, q, a):
-            n0, width = pieces[q]
-            result = keep.tile([P, width], F32, name=f"result{q}{a}")
-            if engine == "vector":
-                nc.vector.tensor_copy(out=result[:], in_=sums[q, a][:])
-            else:
-                nc.scalar.copy(out=result[:], in_=sums[q, a][:])
-            nc.sync.dma_start(out=out_view[:, a, n0 : n0 + width], in_=result[:])
-
+        after_second_half = SECOND_HALF + TWO_TRIPLES
         mean_on_scalar(0)
         mean_on_scalar(1)
-        measure(3, 0)
-        measure(2, 0)
+        measure(LAST, 0, 0, HALF, UNKEPT)
+        measure(2, 0, KEPT[2], HALF, BESIDE_KEPT)
         spread_on_scalar(0)
         mean_on_scalar(2)
-        measure(0, 1)
+        measure(0, 1, 0, HALF, SECOND_HALF)
         spread_on_scalar(1)
-        measure(1, 1)
-        aggregate(0)
+        measure(1, 1, 0, HALF, SECOND_HALF)
+        aggregate(0, SCALAR_TRIPLE, after_second_half)
         spread_on_scalar(2)
-        measure(2, 1)
-        aggregate(1)
-        aggregate(2)
-        measure_last(0)
-        measure_last(1)
-        aggregate(3)
-        roots(3, 1)
-        shift(3)
-        roots(2, 1)
-        shift(2)
-        combine(2)
-        roots(0, 1)
-        shift(0)
-        combine(0)
-        roots(1, 1)
-        shift(1)
-        combine(1)
-        gain_copy(3)
-        normalise("gained", 3, 0, 128)
-        normalise("copy", 2, 0, 256)
-        normalise("copy", 0, 0, 256)
-        normalise("copy", 1, 0, 256)
-        normalise("gained", 3, 128, 128)
-        combine(3)
-        weave("vector", 0)
-        weave("vector", 1)
-        multiply(0)
-        store("scalar", 0)
-        normalise("copy", 0, 256, 256)
-        normalise("copy", 1, 256, 256)
-        normalise("scalar", 2, 256, 256)
-        normalise("scalar", 3, 256, 256)
-        weave("vector", 2)
-        multiply(1)
-        store("scalar", 1)
-        normalise("scalar", 0, 512, 128)
-        normalise("scalar", 0, 640, 128)
-        normalise("scalar", 1, 512, 128)
-        normalise("scalar", 1, 640, 128)
-        normalise("scalar", 2, 512, 256)
-        normalise("scalar", 3, 512, 256)
-        weave("vector", 3)
-        multiply(2)
-        store("scalar", 2)
-        normalise("scalar", 0, 768, 128)
-        normalise("scalar", 0, 896, 128)
-        normalise("scalar", 1, 768, 256)
-        normalise("scalar", 2, 768, 256)
-        normalise("scalar", 3, 768, 256)
-        weave("vector", 4)
-        multiply(3)
-        store("scalar", 3)
-        weave("vector", 5)
-        multiply(4)
-        store("scalar", 4)
-        weave("vector", 6)
-        multiply(5)
-        store("scalar", 5)
-        weave("vector", 7)
-        multiply_split(6, 5, 0)
-        multiply_split(7, 7, 2)
-        store_half("scalar", 6, 0)
-        store_half("vector", 6, 1)
-        store_half("scalar", 7, 0)
-        store_half("vector", 7, 1)
+        measure(2, 1, 0, HALF, SECOND_HALF)
+        aggregate(1, SCALAR_TRIPLE, after_second_half)
+        aggregate(2, BESIDE_KEPT, after_second_half)
+        measure(LAST, 1, 0, QUARTER, SECOND_HALF)
+        measure(LAST, 1, QUARTER, HALF, after_second_half)
+        aggregate(LAST, UNKEPT, after_second_half + TWO_TRIPLES)
+
+        root(LAST)
+        shift(LAST)
+        for t in (2, 0, 1):
+            root(t)
+            shift(t)
+            combine(t)
+        nc.scalar.activation(
+            out=gained[:], in_=banks[LAST, 0][:, 0:QUARTER], func=ACT.Copy, scale=gain[:, LAST : LAST + 1]
+        )
+
+        normalise_gained(0, PIECE)
+        for t in (2, 0, 1):
+            normalise_kept(t, 0, QUARTER)
+        normalise_gained(PIECE, PIECE)
+        combine(LAST)
+
+        def second_quarter():
+            for t in (0, 1):
+                normalise_kept(t, QUARTER, QUARTER)
+            for t in (2, 3):
+                normalise_bank(t, QUARTER, QUARTER)
+
+        def late_quarter(n0, early_tiles):
+            for t in range(PACK):
+                width = PIECE if t in early_tiles else QUARTER
+                for start in range(n0, n0 + QUARTER, width):
+                    normalise_bank(t, start, width)
+
+        behind_store = {
+            0: second_quarter,
+            1: lambda: late_quarter(HALF, (0, 1)),
+            2: lambda: late_quarter(HALF + QUARTER, (0,)),
+        }
+        interleave(0)
+        for q in range(PIECES - len(SPLIT_BANKS)):
+            interleave(q + 1)
+            multiply(q)
+            store(q)
+            if q in behind_store:
+                behind_store[q]()
+        interleave(PIECES - 1)
+        for q in SPLIT_BANKS:
+            multiply(q)
+        for q in SPLIT_BANKS:
+            store_halves(q)

@@ -105,18 +105,6 @@ def tile_picked_inorm_relu_p_kernel(
         minus_gain = keep.tile([P, PACK], F32, name="minus_gain")
         nc.scalar.activation(out=minus_gain[:], in_=gain[:], func=ACT.Copy, scale=-1.0)
 
-        idle = psum.tile([P, HALF], F32, name="idle", tag="bank7")
-        for turn in range(3):
-            nc.tensor.matmul_mx(
-                out=idle[:],
-                lhsT=w1_codes[:, 0:P].bitcast(FP8X4),
-                lhsT_scale=w1_plane[:, 0:P],
-                rhs=w1_codes[:].bitcast(FP8X4),
-                rhs_scale=w1_plane[:],
-                start=True,
-                stop=True,
-            )
-
         banks = {}
         for t, h in ((0, 0), (3, 0), (1, 0), (2, 0), (0, 1), (1, 1), (2, 1), (3, 1)):
             bank = psum.tile([P, HALF], F32, name=f"h{t}{h}", tag=f"bank{2 * t + h}")

@@ -23,6 +23,7 @@ QUARTER = 256
 PIECE = 128
 PIECES = S // PIECE
 LINE = 8
+WARM_ROWS = 32
 LAST = PACK - 1
 KEPT = {0: HALF, 1: HALF, 2: QUARTER}
 BESIDE_KEPT, UNKEPT, SCALAR_TRIPLE, SECOND_HALF = 0, 3, 6, 9
@@ -104,6 +105,18 @@ def tile_picked_inorm_relu_p_kernel(
         nc.scalar.activation(out=factors[:, :, 1], in_=gain[:], func=ACT.Copy)
         minus_gain = keep.tile([P, PACK], F32, name="minus_gain")
         nc.scalar.activation(out=minus_gain[:], in_=gain[:], func=ACT.Copy, scale=-1.0)
+
+        idle = psum.tile([P, HALF], F32, name="idle", tag="bank7")
+        for turn in range(3):
+            nc.tensor.matmul_mx(
+                out=idle[0:WARM_ROWS, :],
+                lhsT=w1_codes[:, 0:WARM_ROWS].bitcast(FP8X4),
+                lhsT_scale=w1_plane[:, 0:WARM_ROWS],
+                rhs=w1_codes[:].bitcast(FP8X4),
+                rhs_scale=w1_plane[:],
+                start=True,
+                stop=True,
+            )
 
         banks = {}
         for t, h in ((0, 0), (3, 0), (1, 0), (2, 0), (0, 1), (1, 1), (2, 1), (3, 1)):

@@ -63,7 +63,9 @@ def tile_picked_inorm_relu_p_kernel(
         nc.sync.dma_start(out=xs_table[32:96:4, :].bitcast(I32), in_=x_scales[0].bitcast(I32))
         nc.sync.dma_start(out=xw_table[:], in_=x_words[0].rearrange("p n r -> p (n r)").bitcast(I32))
         nc.sync.dma_start(out=gain[:], in_=gamma.rearrange("(p t) o -> p (t o)", t=PACK))
-        nc.sync.dma_start(out=w2_codes[:], in_=w2_words[0].rearrange("p n r -> p (n r)").bitcast(I32))
+        w2_in = w2_words[0].rearrange("p n r -> p (n r)").bitcast(I32)
+        for a in range(2):
+            nc.sync.dma_start(out=w2_codes[:, P * a : P * (a + 1)], in_=w2_in[:, P * a : P * (a + 1)])
 
         xs_picked = keep.tile([P, S], U8, name="xs_picked", align_bytes=64)
         nc.vector.tensor_copy(out=xs_picked[:], in_=xs_table[:].indirect(offsets[:]))
@@ -236,14 +238,19 @@ def tile_picked_inorm_relu_p_kernel(
 
         def store(q):
             result = keep.tile([P, 2, PIECE], F32, name=f"result{q}")
-            nc.scalar.copy(out=result[:], in_=sums[q][:])
-            nc.sync.dma_start(out=out_view[:, :, PIECE * q : PIECE * (q + 1)], in_=result[:])
+            parts = ((0, 1), (1, 2)) if q == len(PIECE_BANK) - 1 else ((0, 2),)
+            for a0, a1 in parts:
+                nc.scalar.copy(out=result[:, a0:a1, :], in_=sums[q][:, a0:a1, :])
+                nc.sync.dma_start(out=out_view[:, a0:a1, PIECE * q : PIECE * (q + 1)], in_=result[:, a0:a1, :])
 
-        def store_halves(q):
-            for a, copy in enumerate((nc.scalar.copy, nc.vector.tensor_copy)):
-                result = keep.tile([P, PIECE], F32, name=f"result{q}{a}")
-                copy(out=result[:], in_=sums[q, a][:])
-                nc.sync.dma_start(out=out_view[:, a, PIECE * q : PIECE * (q + 1)], in_=result[:])
+        def store_last_pair():
+            first = PIECE * min(SPLIT_BANKS)
+            results = [keep.tile([P, len(SPLIT_BANKS), PIECE], F32, name=f"last{a}") for a in range(2)]
+            for place, q in enumerate(SPLIT_BANKS):
+                for a, copy in enumerate((nc.scalar.copy, nc.vector.tensor_copy)):
+                    copy(out=results[a][:, place, :], in_=sums[q, a][:])
+            for a in range(2):
+                nc.sync.dma_start(out=out_view[:, a, first:S], in_=results[a][:].rearrange("p q n -> p (q n)"))
 
         after_second_half = SECOND_HALF + TWO_TRIPLES
         mean_on_scalar(0)
@@ -307,5 +314,4 @@ def tile_picked_inorm_relu_p_kernel(
         interleave(PIECES - 1)
         for q in SPLIT_BANKS:
             multiply(q)
-        for q in SPLIT_BANKS:
-            store_halves(q)
+        store_last_pair()

@@ -44,15 +44,13 @@ def tile_picked_inorm_relu_p_kernel(
         xs_table = keep.tile([P, T], U8, name="xs_table", tag="scale_rows", align_bytes=64)
         xw_table = keep.tile([P, T], I32, name="xw_table", align_bytes=64)
         w1_raw = keep.tile([P, PACK, H], F32, name="w1_raw", align_bytes=64)
-        w2_codes = keep.tile([P, N], I32, name="w2_codes", align_bytes=64)
         gain = keep.tile([P, PACK], F32, name="gain")
 
         xs = keep.tile([P, S], U8, name="xs", align_bytes=64)
-        nc.vector.memset(xs_table[:].bitcast(I32), 0)
-        nc.vector.memset(xs[:].bitcast(I32), 0)
-
         w2_plane = keep.tile([P, N], U8, name="w2_plane", align_bytes=64)
         nc.vector.memset(w2_plane[:].bitcast(I32), 0)
+        nc.vector.memset(xs_table[:].bitcast(I32), 0)
+        nc.vector.memset(xs[:].bitcast(I32), 0)
 
         warm = keep.tile([P, 2], F32, name="warm")
         nc.vector.memset(warm[:, 0:1], 1.0)
@@ -60,26 +58,27 @@ def tile_picked_inorm_relu_p_kernel(
 
         nc.sync.dma_start(out=w1_raw[:], in_=w1.rearrange("(p j) c -> p j c", j=PACK))
         nc.sync.dma_start(out=offsets[:], in_=offs)
-        nc.sync.dma_start(out=xs_table[32:96:4, :].bitcast(I32), in_=x_scales[0].bitcast(I32))
-        nc.sync.dma_start(out=xw_table[:], in_=x_words[0].rearrange("p n r -> p (n r)").bitcast(I32))
-        nc.sync.dma_start(out=gain[:], in_=gamma.rearrange("(p t) o -> p (t o)", t=PACK))
-        w2_in = w2_words[0].rearrange("p n r -> p (n r)").bitcast(I32)
-        for a in range(2):
-            nc.sync.dma_start(out=w2_codes[:, P * a : P * (a + 1)], in_=w2_in[:, P * a : P * (a + 1)])
-
-        xs_picked = keep.tile([P, S], U8, name="xs_picked", align_bytes=64)
-        nc.vector.tensor_copy(out=xs_picked[:], in_=xs_table[:].indirect(offsets[:]))
-        for q in range(4):
-            nc.scalar.dma_start(
-                out=xs[32 * q : 32 * q + 4, :].bitcast(I32),
-                in_=xs_picked[32 + 16 * q : 48 + 16 * q : 4, :].bitcast(I32),
-            )
-
         for q in range(4):
             nc.sync.dma_start(
                 out=w2_plane[32 * q : 32 * q + 4, :].bitcast(I32),
                 in_=w2_scales[0, 4 * q : 4 * q + 4, :].bitcast(I32),
             )
+        nc.sync.dma_start(out=xs_table[32:96:4, :].bitcast(I32), in_=x_scales[0].bitcast(I32))
+        nc.sync.dma_start(out=xw_table[:], in_=x_words[0].rearrange("p n r -> p (n r)").bitcast(I32))
+        nc.sync.dma_start(out=gain[:], in_=gamma.rearrange("(p t) o -> p (t o)", t=PACK))
+
+        xs_picked = keep.tile([P, S], U8, name="xs_picked", tag="picked", align_bytes=64)
+        nc.vector.tensor_copy(out=xs_picked[:], in_=xs_table[:].indirect(offsets[:]))
+        for q in range(4):
+            nc.sync.dma_start(
+                out=xs[32 * q : 32 * q + 4, :].bitcast(I32),
+                in_=xs_picked[32 + 16 * q : 48 + 16 * q : 4, :].bitcast(I32),
+            )
+
+        w2_codes = keep.tile([P, N], I32, name="w2_codes", tag="picked", align_bytes=64)
+        w2_in = w2_words[0].rearrange("p n r -> p (n r)").bitcast(I32)
+        for a in range(2):
+            nc.sync.dma_start(out=w2_codes[:, P * a : P * (a + 1)], in_=w2_in[:, P * a : P * (a + 1)])
 
         w1_grouped = keep.tile([P, PACK, P, PACK], BF16, name="w1_grouped", align_bytes=64)
         w1_dst = w1_grouped[:].rearrange("p t m j -> p m t j")

@@ -47,8 +47,6 @@ def tile_picked_inorm_relu_p_kernel(
         gain = keep.tile([P, PACK], F32, name="gain")
 
         xs = keep.tile([P, S], U8, name="xs", align_bytes=64)
-        w2_plane = keep.tile([P, N], U8, name="w2_plane", align_bytes=64)
-        nc.vector.memset(w2_plane[:].bitcast(I32), 0)
         nc.vector.memset(xs_table[:].bitcast(I32), 0)
         nc.vector.memset(xs[:].bitcast(I32), 0)
 
@@ -58,11 +56,6 @@ def tile_picked_inorm_relu_p_kernel(
 
         nc.sync.dma_start(out=w1_raw[:], in_=w1.rearrange("(p j) c -> p j c", j=PACK))
         nc.sync.dma_start(out=offsets[:], in_=offs)
-        for q in range(4):
-            nc.sync.dma_start(
-                out=w2_plane[32 * q : 32 * q + 4, :].bitcast(I32),
-                in_=w2_scales[0, 4 * q : 4 * q + 4, :].bitcast(I32),
-            )
         nc.sync.dma_start(out=xs_table[32:96:4, :].bitcast(I32), in_=x_scales[0].bitcast(I32))
         nc.sync.dma_start(out=xw_table[:], in_=x_words[0].rearrange("p n r -> p (n r)").bitcast(I32))
         nc.sync.dma_start(out=gain[:], in_=gamma.rearrange("(p t) o -> p (t o)", t=PACK))
@@ -80,7 +73,7 @@ def tile_picked_inorm_relu_p_kernel(
         for a in range(2):
             nc.sync.dma_start(out=w2_codes[:, P * a : P * (a + 1)], in_=w2_in[:, P * a : P * (a + 1)])
 
-        w1_grouped = keep.tile([P, PACK, P, PACK], BF16, name="w1_grouped", align_bytes=64)
+        w1_grouped = keep.tile([P, PACK, P, PACK], BF16, name="w1_grouped", tag="grouped", align_bytes=64)
         w1_dst = w1_grouped[:].rearrange("p t m j -> p m t j")
         w1_src = w1_raw[:].rearrange("p j (m t) -> p m t j", t=PACK)
         nc.scalar.copy(out=w1_dst, in_=w1_src)
@@ -91,6 +84,14 @@ def tile_picked_inorm_relu_p_kernel(
             scales=w1_plane[:],
             in_=w1_grouped[:].rearrange("p t m j -> p (t m j)"),
         )
+
+        w2_plane = keep.tile([P, N], U8, name="w2_plane", tag="grouped", align_bytes=64)
+        nc.vector.memset(w2_plane[:].bitcast(I32), 0)
+        for q in range(4):
+            nc.sync.dma_start(
+                out=w2_plane[32 * q : 32 * q + 4, :].bitcast(I32),
+                in_=w2_scales[0, 4 * q : 4 * q + 4, :].bitcast(I32),
+            )
 
         xw = []
         for h in range(2):

@@ -59,19 +59,18 @@ def tile_picked_inorm_relu_p_kernel(
         nc.sync.dma_start(out=xs_table[32:96:4, :].bitcast(I32), in_=x_scales[0].bitcast(I32))
         nc.sync.dma_start(out=xw_table[:], in_=x_words[0].rearrange("p n r -> p (n r)").bitcast(I32))
         nc.sync.dma_start(out=gain[:], in_=gamma.rearrange("(p t) o -> p (t o)", t=PACK))
-
-        xs_picked = keep.tile([P, S], U8, name="xs_picked", tag="picked", align_bytes=64)
-        nc.vector.tensor_copy(out=xs_picked[:], in_=xs_table[:].indirect(offsets[:]))
-        for q in range(4):
-            nc.sync.dma_start(
-                out=xs[32 * q : 32 * q + 4, :].bitcast(I32),
-                in_=xs_picked[32 + 16 * q : 48 + 16 * q : 4, :].bitcast(I32),
-            )
-
-        w2_codes = keep.tile([P, N], I32, name="w2_codes", tag="picked", align_bytes=64)
+        w2_codes = keep.tile([P, N], I32, name="w2_codes", align_bytes=64)
         w2_in = w2_words[0].rearrange("p n r -> p (n r)").bitcast(I32)
         for a in range(2):
             nc.sync.dma_start(out=w2_codes[:, P * a : P * (a + 1)], in_=w2_in[:, P * a : P * (a + 1)])
+
+        xs_picked = keep.tile([P, S], U8, name="xs_picked", align_bytes=64)
+        nc.vector.tensor_copy(out=xs_picked[:], in_=xs_table[:].indirect(offsets[:]))
+        for q in range(4):
+            nc.scalar.dma_start(
+                out=xs[32 * q : 32 * q + 4, :].bitcast(I32),
+                in_=xs_picked[32 + 16 * q : 48 + 16 * q : 4, :].bitcast(I32),
+            )
 
         w1_grouped = keep.tile([P, PACK, P, PACK], BF16, name="w1_grouped", tag="grouped", align_bytes=64)
         w1_dst = w1_grouped[:].rearrange("p t m j -> p m t j")

from contextlib import ExitStack

import concourse.mybir as mybir

K, T, S, H, N = 512, 4096, 1024, 512, 256
FLOPS = 2 * K * H * S + 2 * H * N * S
EPS = 1e-5

F32 = mybir.dt.float32
BF16 = mybir.dt.bfloat16
I32 = mybir.dt.int32
U32 = mybir.dt.uint32
U16 = mybir.dt.uint16
U8 = mybir.dt.uint8
FP8X4 = mybir.dt.float8_e4m3fn_x4
ACT = mybir.ActivationFunctionType
ALU = mybir.AluOpType

P = 128
PACK = 4
HALF = 512
QUARTER = 256
PIECE = 128
PIECES = S // PIECE
LINE = 8
WARM_ROWS = 32
LAST = PACK - 1
KEPT = {0: HALF, 1: HALF, 2: QUARTER}
BESIDE_KEPT, UNKEPT, SCALAR_TRIPLE, SECOND_HALF = 0, 3, 6, 9
TWO_TRIPLES = 6
PIECE_BANK = (0, 2, 4, 6, 1, 3)
SPLIT_BANKS = {6: (5, 0), 7: (7, 2)}


def tile_picked_inorm_relu_p_kernel(
    tc, x_words, x_scales, w1, w2_words, w2_scales, gamma, offs, out
):
    nc = tc.nc
    with ExitStack() as ctx:
        keep = ctx.enter_context(tc.tile_pool(name="keep", bufs=1))
        psum = ctx.enter_context(tc.psum_pool(name="psum", bufs=1))

        offsets = keep.tile([P, S // 16], U16, name="offsets")
        xs_table = keep.tile([P, T], U8, name="xs_table", tag="scale_rows", align_bytes=64)
        xw_table = keep.tile([P, T], I32, name="xw_table", align_bytes=64)
        w1_raw = keep.tile([P, PACK, H], F32, name="w1_raw", align_bytes=64)
        gain = keep.tile([P, PACK], F32, name="gain")

        xs = keep.tile([P, S], U8, name="xs", align_bytes=64)
        nc.vector.memset(xs_table[:].bitcast(I32), 0)
        nc.vector.memset(xs[:].bitcast(I32), 0)

        warm = keep.tile([P, 2], F32, name="warm")
        nc.vector.memset(warm[:, 0:1], 1.0)
        nc.scalar.activation(out=warm[:, 1:2], in_=warm[:, 0:1], func=ACT.Abs_reciprocal_sqrt, bias=EPS)

        nc.sync.dma_start(out=w1_raw[:], in_=w1.rearrange("(p j) c -> p j c", j=PACK))
        nc.sync.dma_start(out=offsets[:], in_=offs)
        nc.sync.dma_start(out=xs_table[32:96:4, :].bitcast(I32), in_=x_scales[0].bitcast(I32))
        nc.sync.dma_start(out=xw_table[:], in_=x_words[0].rearrange("p n r -> p (n r)").bitcast(I32))
        nc.sync.dma_start(out=gain[:], in_=gamma.rearrange("(p t) o -> p (t o)", t=PACK))
        w2_codes = keep.tile([P, N], I32, name="w2_codes", align_bytes=64)
        w2_in = w2_words[0].rearrange("p n r -> p (n r)").bitcast(I32)
        for a in range(2):
            nc.sync.dma_start(out=w2_codes[:, P * a : P * (a + 1)], in_=w2_in[:, P * a : P * (a + 1)])

        xs_picked = keep.tile([P, S], U8, name="xs_picked", align_bytes=64)
        nc.vector.tensor_copy(out=xs_picked[:], in_=xs_table[:].indirect(offsets[:]))
        for q in range(4):
            nc.scalar.dma_start(
                out=xs[32 * q : 32 * q + 4, :].bitcast(I32),
                in_=xs_picked[32 + 16 * q : 48 + 16 * q : 4, :].bitcast(I32),
            )

        w1_grouped = keep.tile([P, PACK, P, PACK], BF16, name="w1_grouped", tag="grouped", align_bytes=64)
        w1_dst = w1_grouped[:].rearrange("p t m j -> p m t j")
        w1_src = w1_raw[:].rearrange("p j (m t) -> p m t j", t=PACK)
        nc.scalar.copy(out=w1_dst, in_=w1_src)
        w1_codes = keep.tile([P, H], U32, name="w1_codes", tag="scale_rows", align_bytes=64)
        w1_plane = keep.tile([P, H], U8, name="w1_plane", align_bytes=64)
        nc.vector.quantize_mx(
            out=w1_codes[:].bitcast(FP8X4),
            scales=w1_plane[:],
            in_=w1_grouped[:].rearrange("p t m j -> p (t m j)"),
        )

        w2_plane = keep.tile([P, N], U8, name="w2_plane", tag="grouped", align_bytes=64)
        nc.vector.memset(w2_plane[:].bitcast(I32), 0)
        for q in range(4):
            nc.sync.dma_start(
                out=w2_plane[32 * q : 32 * q + 4, :].bitcast(I32),
                in_=w2_scales[0, 4 * q : 4 * q + 4, :].bitcast(I32),
            )

        xw = []
        for h in range(2):
            picked = keep.tile([P, HALF], U32, name=f"xw{h}", align_bytes=64)
            nc.vector.tensor_copy(
                out=picked[:], in_=xw_table[:].bitcast(U32).indirect(offsets[:, 32 * h : 32 * (h + 1)])
            )
            xw.append(picked)

        factors = keep.tile([P, PACK, 3], F32, name="factors")
        for t, width in KEPT.items():
            nc.scalar.activation(out=factors[:, t, 0:1], in_=gain[:, t : t + 1], func=ACT.Copy, scale=float(width))
        nc.scalar.activation(out=factors[:, :, 1], in_=gain[:], func=ACT.Copy)
        minus_gain = keep.tile([P, PACK], F32, name="minus_gain")
        nc.scalar.activation(out=minus_gain[:], in_=gain[:], func=ACT.Copy, scale=-1.0)

        idle = psum.tile([P, HALF], F32, name="idle", tag="bank7")
        for turn in range(3):
            nc.tensor.matmul_mx(
                out=idle[0:WARM_ROWS, :],
                lhsT=w1_codes[:, 0:WARM_ROWS].bitcast(FP8X4),
                lhsT_scale=w1_plane[:, 0:WARM_ROWS],
                rhs=w1_codes[:].bitcast(FP8X4),
                rhs_scale=w1_plane[:],
                start=True,
                stop=True,
            )

        banks = {}
        for t, h in ((0, 0), (3, 0), (1, 0), (2, 0), (0, 1), (1, 1), (2, 1), (3, 1)):
            bank = psum.tile([P, HALF], F32, name=f"h{t}{h}", tag=f"bank{2 * t + h}")
            for c0 in (0, QUARTER):
                nc.tensor.matmul_mx(
                    out=bank[:, c0 : c0 + QUARTER],
                    lhsT=w1_codes[:, P * t : P * (t + 1)].bitcast(FP8X4),
                    lhsT_scale=w1_plane[:, P * t : P * (t + 1)],
                    rhs=xw[h][:, c0 : c0 + QUARTER].bitcast(FP8X4),
                    rhs_scale=xs[:, HALF * h + c0 : HALF * h + c0 + QUARTER],
                    start=True,
                    stop=True,
                )
            banks[t, h] = bank

        z_rows = [keep.tile([P, PACK, HALF], BF16, name=f"z_rows{h}", align_bytes=64) for h in range(2)]
        stats = keep.tile([P, PACK, 24], F32, name="stats")
        squares = keep.tile([P, PACK, HALF], BF16, name="squares")
        shrunk = {t: keep.tile([P, width], F32, name=f"shrunk{t}") for t, width in KEPT.items()}
        moments = keep.tile([P, PACK, 2], F32, name="moments")
        rstd = keep.tile([P, PACK], F32, name="rstd")
        gained = keep.tile([P, QUARTER], F32, name="gained")
        affine = [keep.tile([P, 3], F32, name=f"affine{t}") for t in range(PACK)]
        for t, width in KEPT.items():
            nc.vector.memset(stats[:, t, SCALAR_TRIPLE : SCALAR_TRIPLE + 1], float(width))

        def mean_on_scalar(t):
            nc.scalar.activation(
                out=shrunk[t][:], in_=banks[t, 0][:, 0 : KEPT[t]], func=ACT.Identity,
                scale=1.0 / KEPT[t], accum_out=stats[:, t, SCALAR_TRIPLE + 1 : SCALAR_TRIPLE + 2],
            )

        def spread_on_scalar(t):
            nc.scalar.activation(
                out=squares[:, t, 0 : KEPT[t]], in_=shrunk[t][:], func=ACT.Square,
                scale=-float(KEPT[t]), bias=stats[:, t, SCALAR_TRIPLE + 1 : SCALAR_TRIPLE + 2],
                accum_out=stats[:, t, SCALAR_TRIPLE + 2 : SCALAR_TRIPLE + 3],
            )

        def measure(t, h, c0, c1, column):
            nc.vector.bn_stats(out=stats[:, t, column : column + TWO_TRIPLES], in_=banks[t, h][:, c0:c1])

        def aggregate(t, first, last):
            nc.vector.bn_aggr(out=moments[:, t, :], in_=stats[:, t, first:last])

        def root(t):
            nc.scalar.activation(
                out=rstd[:, t : t + 1], in_=moments[:, t : t + 1, 1], func=ACT.Abs_reciprocal_sqrt, bias=EPS
            )

        def shift(t):
            nc.scalar.activation(
                out=factors[:, t, 2:3], in_=moments[:, t, 0:1], func=ACT.Copy, scale=minus_gain[:, t : t + 1]
            )

        def combine(t):
            first = 0 if t in KEPT else 1
            nc.scalar.activation(
                out=affine[t][:, first:3], in_=factors[:, t, first:3], func=ACT.Copy, scale=rstd[:, t : t + 1]
            )

        def z_slice(t, n0, width):
            h, c0 = divmod(n0, HALF)
            return z_rows[h][:, t, c0 : c0 + width]

        def normalise_bank(t, n0, width):
            h, c0 = divmod(n0, HALF)
            nc.scalar.activation(
                out=z_slice(t, n0, width), in_=banks[t, h][:, c0 : c0 + width], func=ACT.Relu,
                scale=affine[t][:, 1:2], bias=affine[t][:, 2:3],
            )

        def normalise_kept(t, n0, width):
            nc.vector.tensor_scalar(
                out=z_slice(t, n0, width), in0=shrunk[t][:, n0 : n0 + width],
                scalar1=affine[t][:, 0:1], scalar2=affine[t][:, 2:3], op0=ALU.mult, op1=ALU.add,
            )

        def normalise_gained(n0, width):
            nc.vector.tensor_scalar(
                out=z_slice(LAST, n0, width), in0=gained[:, n0 : n0 + width],
                scalar1=factors[:, LAST, 2:3], scalar2=rstd[:, LAST : LAST + 1], op0=ALU.add, op1=ALU.mult,
            )

        out_view = out.rearrange("(a p) n -> p a n", p=P)
        grouped = {}
        sums = {}

        def interleave(q):
            h, c0 = divmod(PIECE * q, HALF)
            grouped[q] = keep.tile([P, PIECE, PACK], BF16, name=f"z_grouped{q}", align_bytes=64)
            dst = grouped[q][:].rearrange("p (c i) t -> p c t i", i=LINE)
            src = z_rows[h][:, :, c0 : c0 + PIECE].rearrange("p t (c i) -> p c t i", i=LINE)
            nc.vector.tensor_scalar(out=dst, in0=src, scalar1=0.0, scalar2=None, op0=ALU.max)

        def multiply(q):
            z_codes = keep.tile([P, PIECE], U32, name=f"z_codes{q}", align_bytes=64)
            z_plane = keep.tile([P, PIECE], U8, name=f"z_plane{q}", align_bytes=64)
            nc.vector.quantize_mx(
                out=z_codes[:].bitcast(FP8X4), scales=z_plane[:], in_=grouped[q][:].rearrange("p n t -> p (n t)")
            )
            if q not in SPLIT_BANKS:
                sums[q] = psum.tile([P, 2, PIECE], F32, name=f"acc{q}", tag=f"bank{PIECE_BANK[q]}")
            for a in range(2):
                if q in SPLIT_BANKS:
                    sums[q, a] = psum.tile([P, PIECE], F32, name=f"acc{q}{a}", tag=f"bank{SPLIT_BANKS[q][a]}")
                nc.tensor.matmul_mx(
                    out=sums[q, a][:] if q in SPLIT_BANKS else sums[q][:, a, :],
                    lhsT=w2_codes[:, P * a : P * (a + 1)].bitcast(FP8X4),
                    lhsT_scale=w2_plane[:, P * a : P * (a + 1)],
                    rhs=z_codes[:].bitcast(FP8X4),
                    rhs_scale=z_plane[:],
                    start=True,
                    stop=True,
                )

        def store(q):
            result = keep.tile([P, 2, PIECE], F32, name=f"result{q}")
            parts = ((0, 1), (1, 2)) if q == len(PIECE_BANK) - 1 else ((0, 2),)
            for a0, a1 in parts:
                nc.scalar.copy(out=result[:, a0:a1, :], in_=sums[q][:, a0:a1, :])
                nc.sync.dma_start(out=out_view[:, a0:a1, PIECE * q : PIECE * (q + 1)], in_=result[:, a0:a1, :])

        def store_last_pair():
            first = PIECE * min(SPLIT_BANKS)
            results = [keep.tile([P, len(SPLIT_BANKS), PIECE], F32, name=f"last{a}") for a in range(2)]
            for place, q in enumerate(SPLIT_BANKS):
                for a, copy in enumerate((nc.scalar.copy, nc.vector.tensor_copy)):
                    copy(out=results[a][:, place, :], in_=sums[q, a][:])
            for a in range(2):
                nc.sync.dma_start(out=out_view[:, a, first:S], in_=results[a][:].rearrange("p q n -> p (q n)"))

        after_second_half = SECOND_HALF + TWO_TRIPLES
        mean_on_scalar(0)
        mean_on_scalar(1)
        measure(LAST, 0, 0, HALF, UNKEPT)
        measure(2, 0, KEPT[2], HALF, BESIDE_KEPT)
        spread_on_scalar(0)
        mean_on_scalar(2)
        measure(0, 1, 0, HALF, SECOND_HALF)
        spread_on_scalar(1)
        measure(1, 1, 0, HALF, SECOND_HALF)
        aggregate(0, SCALAR_TRIPLE, after_second_half)
        spread_on_scalar(2)
        measure(2, 1, 0, HALF, SECOND_HALF)
        aggregate(1, SCALAR_TRIPLE, after_second_half)
        aggregate(2, BESIDE_KEPT, after_second_half)
        measure(LAST, 1, 0, QUARTER, SECOND_HALF)
        measure(LAST, 1, QUARTER, HALF, after_second_half)
        aggregate(LAST, UNKEPT, after_second_half + TWO_TRIPLES)

        root(LAST)
        shift(LAST)
        for t in (2, 0, 1):
            root(t)
            shift(t)
            combine(t)
        nc.scalar.activation(
            out=gained[:], in_=banks[LAST, 0][:, 0:QUARTER], func=ACT.Copy, scale=gain[:, LAST : LAST + 1]
        )

        normalise_gained(0, PIECE)
        for t in (2, 0, 1):
            normalise_kept(t, 0, QUARTER)
        normalise_gained(PIECE, PIECE)
        combine(LAST)

        def second_quarter():
            for t in (0, 1):
                normalise_kept(t, QUARTER, QUARTER)
            for t in (2, 3):
                normalise_bank(t, QUARTER, QUARTER)

        def late_quarter(n0, early_tiles):
            for t in range(PACK):
                width = PIECE if t in early_tiles else QUARTER
                for start in range(n0, n0 + QUARTER, width):
                    normalise_bank(t, start, width)

        behind_store = {
            0: second_quarter,
            1: lambda: late_quarter(HALF, (0, 1)),
            2: lambda: late_quarter(HALF + QUARTER, (0,)),
        }
        interleave(0)
        for q in range(PIECES - len(SPLIT_BANKS)):
            interleave(q + 1)
            multiply(q)
            store(q)
            if q in behind_store:
                behind_store[q]()
        interleave(PIECES - 1)
        for q in SPLIT_BANKS:
            multiply(q)
        store_last_pair()
